import numpy as np
import ml_dtypes


def mxq(x, axis, fmt="e4m3"):
    dtype, down = {"e4m3": (ml_dtypes.float8_e4m3fn, 7), "e5m2": (ml_dtypes.float8_e5m2, 14)}[fmt]
    v = np.moveaxis(np.asarray(x, np.float32).astype(ml_dtypes.bfloat16).astype(np.float64), axis, -1)
    blocks = v.reshape(v.shape[:-1] + (-1, 32))
    amax = np.abs(blocks).max(-1, keepdims=True)
    byte = np.maximum(np.where(amax > 0, np.frexp(amax)[1] - 1 + 127, 0) - down, 1)
    scale = np.exp2(byte - 127.0)
    codes = (blocks / scale).astype(np.float32).astype(dtype).astype(np.float64)
    return np.moveaxis((codes * scale).reshape(v.shape), -1, axis)


WIDE = False


def mx_kscale(k):
    if not WIDE:
        return np.ones(k)
    levels = np.array([10, -10, 5, -5, 0])
    if k % 512:
        return np.exp2(np.random.permutation(np.resize(levels, k // 32))).repeat(32)
    a = np.empty((k // 512, 16))
    for p in range(k // 512):
        a[p, :8] = np.random.permutation(np.resize(levels, 8))
        for g in range(8):
            far = levels[np.abs(levels - a[p, g]) >= 10]
            a[p, g + 8] = far[np.random.randint(len(far))]
    return np.exp2(a.ravel()).repeat(32)


def f64(x):
    return np.asarray(x).astype(np.float64)


def striped(idx):
    return np.tile(np.asarray(idx).reshape(-1, 16).T, (8, 1)).astype(np.uint16)


def unstriped(offs):
    return offs[:16].T.reshape(-1).astype(np.int64)


E2M1 = np.array([0.0, 0.5, 1.0, 1.5, 2.0, 3.0, 4.0, 6.0, -0.0, -0.5, -1.0, -1.5, -2.0, -3.0, -4.0, -6.0])


def pack_weight(w, fmt):
    k, n = w.shape
    w = f64(np.asarray(w, np.float32).astype(ml_dtypes.bfloat16)).reshape(k // 32, 32, n)
    amax = np.abs(w).max(1)
    if fmt == "e4m3":
        byte = np.frexp(amax)[1] - 1 + 127 - 7
    else:
        mant, ex = np.frexp(amax / 6.0)
        byte = np.where(mant > 0.5, ex, ex - 1) + 127
    byte = np.clip(np.where(amax > 0, byte, 1), 1, 254)
    scaled = (w * np.exp2(127.0 - byte)[:, None, :]).reshape(k, n).astype(np.float32)
    by_word = np.ascontiguousarray(scaled.reshape(k // 512, 128, 4, n).transpose(0, 1, 3, 2))
    if fmt == "e4m3":
        words = by_word.astype(ml_dtypes.float8_e4m3fn).view(np.uint8)
    else:
        c = by_word.astype(ml_dtypes.float4_e2m1fn).view(np.uint8) & 0xF
        words = (c[..., 0::2] | (c[..., 1::2] << 4)).reshape(k // 512, 128, 2 * n)
    return np.ascontiguousarray(words), np.ascontiguousarray(byte.astype(np.uint8).reshape(k // 512, 16, n))


def unpack_weight(words, scales, fmt):
    g, _, n = scales.shape
    words = np.ascontiguousarray(words).reshape(g, 128, n, -1)
    if fmt == "e4m3":
        vals = words.view(ml_dtypes.float8_e4m3fn).astype(np.float64)
    else:
        nib = np.empty((g, 128, n, 4), np.uint8)
        nib[..., 0::2] = words & 0xF
        nib[..., 1::2] = words >> 4
        vals = E2M1[nib]
    vals = vals * np.repeat(np.exp2(scales.astype(np.float64) - 127.0), 8, axis=1)[..., None]
    return vals.transpose(0, 1, 3, 2).reshape(g * 512, n)


def sigmoid(v):
    return 1.0 / (1.0 + np.exp(-v))


D, T, I, Q, E, M = 512, 2048, 512, 128, 512, 512


def setup_inputs():
    n = np.random.standard_normal
    idx = np.random.permutation(T)[:I]
    fd = mx_kscale(D)
    fm = mx_kscale(M)
    fi = mx_kscale(I)
    ti = np.ones(T)
    ti[idx] = fi
    keysp = pack_weight(n((D, T)) / fd[:, None], "e4m3")
    return {
        "query": (n((D, Q)) * 0.4 / np.sqrt(D) * fd[:, None]).astype(np.float32),
        "wkey": (n((D, M)) / fd[:, None]).astype(np.float32),
        "wval": (n((M, E)) / fm[:, None]).astype(np.float32),
        "keys_words": keysp[0],
        "keys_scales": keysp[1],
        "vals": (n((E, T)) / ti).astype(np.float32),
        "gb": (np.random.uniform(-1.5, 1.5, (Q, 1))).astype(np.float32),
        "msz": (np.random.uniform(0.5, 2.0, (1, M)) * fm).astype(np.float32),
        "size": (np.random.uniform(0.5, 2.0, (1, I)) * fi).astype(np.float32),
        "offs": striped(idx),
    }


def reference(query, wkey, wval, keys_words, keys_scales, vals, gb, msz, size, offs):
    idx = unstriped(offs)
    keysu = unpack_weight(keys_words, keys_scales, "e4m3")
    queryq = mxq(f64(query), 0, "e4m3")
    wkeyq = mxq(f64(wkey), 0, "e4m3")
    a = queryq.T @ wkeyq
    keysidxg = keysu[:, idx]
    b = queryq.T @ keysidxg
    g = sigmoid(f64(gb))
    p = np.exp(a - np.max(a, axis=1, keepdims=True))
    w = p * f64(msz) * (1.0 - g) / np.sum(p, axis=1, keepdims=True)
    wt = w.T
    r = np.exp(b - np.max(b, axis=1, keepdims=True))
    x = r * f64(size) * g / np.sum(r, axis=1, keepdims=True)
    xt = x.T
    vt = f64(vals)[:, idx].T
    wtq = mxq(wt, 0, "e4m3")
    wvalq = mxq(f64(wval), 0, "e4m3")
    xtq = mxq(xt, 0, "e4m3")
    vtq = mxq(vt, 0, "e4m3")
    o = wtq.T @ wvalq + xtq.T @ vtq
    return o

@@ -1,0 +1,211 @@
+from contextlib import ExitStack
+
+import concourse.mybir as mybir
+from concourse.masks import make_identity
+
+D, T, I, Q, E, M = 512, 2048, 512, 128, 512, 512
+FLOPS = 2 * Q * (D * M + D * I + M * E + I * E)
+
+F32 = mybir.dt.float32
+BF16 = mybir.dt.bfloat16
+I32 = mybir.dt.int32
+U32 = mybir.dt.uint32
+U16 = mybir.dt.uint16
+U8 = mybir.dt.uint8
+FP8X4 = mybir.dt.float8_e4m3fn_x4
+ALU = mybir.AluOpType
+ACT = mybir.ActivationFunctionType
+
+P = 128
+PACK = 4
+BLOCKS = E // P
+GATE_CLAMP = 80.0
+
+
+def interleave(copy, dst, src):
+    copy(out=dst.rearrange("p (c i) t -> p c t i", i=4), in_=src.rearrange("p t (c i) -> p c t i", i=4))
+
+
+def quantize(nc, codes, scales, grouped):
+    nc.vector.quantize_mx(out=codes.bitcast(FP8X4), scales=scales, in_=grouped.rearrange("p c t -> p (c t)"))
+
+
+def tile_attend_knn_memory_kernel(tc, query, wkey, wval, keys_words, keys_scales, vals, gb, msz, size, offs, out):
+    nc = tc.nc
+    with ExitStack() as ctx:
+        keep = ctx.enter_context(tc.tile_pool(name="keep", bufs=1))
+        psum = ctx.enter_context(tc.psum_pool(name="psum", bufs=1))
+
+        def mx_tiles(name, width, tag=None, scale_tag=None):
+            codes = keep.tile([P, width], U32, name=name + "_codes", tag=tag or name + "_codes", align_bytes=64)
+            scales = keep.tile([P, width], U8, name=name + "_scales", tag=scale_tag or name + "_scales", align_bytes=64)
+            return codes, scales
+
+        key_bytes = keep.tile([P, T], U8, name="key_bytes", tag="key_bytes", align_bytes=64)
+        nc.gpsimd.memset(key_bytes[:].bitcast(I32), 0)
+        ident = keep.tile([P, P], F32, name="ident")
+        make_identity(nc, ident[:])
+
+        q_raw = keep.tile([P, PACK, Q], F32, name="q_raw")
+        nc.sync.dma_start(out=q_raw[:], in_=query.rearrange("(p t) c -> p t c", t=PACK))
+        offsets = keep.tile([P, I // 16], U16, name="offsets")
+        nc.sync.dma_start(offsets[:], offs)
+        for quad in range(4):
+            nc.sync.dma_start(
+                out=key_bytes[32 * quad : 32 * quad + 4, :].bitcast(I32),
+                in_=keys_scales[0, 4 * quad : 4 * quad + 4, :].bitcast(I32),
+            )
+        wkey_raw = keep.tile([P, PACK, M], F32, name="wkey_raw", tag="wkey")
+        nc.sync.dma_start(out=wkey_raw[:], in_=wkey.rearrange("(p t) c -> p t c", t=PACK))
+        gate = keep.tile([P, 1], F32, name="gate")
+        nc.sync.dma_start(out=gate[:], in_=gb)
+        msz_col = keep.tile([P, PACK], F32, name="msz_col")
+        nc.sync.dma_start(out=msz_col[:], in_=msz.rearrange("o (p t) -> (o p) t", t=PACK))
+        size_col = keep.tile([P, PACK], F32, name="size_col", tag="size_col", align_bytes=64)
+        nc.sync.dma_start(out=size_col[:], in_=size.rearrange("o (p t) -> (o p) t", t=PACK))
+        key_words = keep.tile([P, T], U32, name="key_words", tag="keys")
+        nc.sync.dma_start(
+            out=key_words[:].bitcast(I32), in_=keys_words[0].rearrange("p n t -> p (n t)").bitcast(I32)
+        )
+        val_raw = {}
+        for b in reversed(range(BLOCKS)):
+            val_raw[b] = keep.tile([P, T], F32, name="val_raw%d" % b, tag="val%d" % b, align_bytes=64)
+            nc.sync.dma_start(out=val_raw[b][:], in_=vals[b * P : (b + 1) * P, :])
+        wval_rows = wval.rearrange("(p t) c -> p t c", t=PACK)
+        wval_raw = {}
+        for h in range(2):
+            wval_raw[h] = keep.tile([P, PACK, 2 * P], F32, name="wval_raw%d" % h, tag="wval%d" % h, align_bytes=64)
+            nc.sync.dma_start(out=wval_raw[h][:], in_=wval_rows[:, :, 2 * P * h : 2 * P * (h + 1)])
+
+        zero = keep.tile([P, 1], F32, name="zero")
+        nc.vector.memset(zero[:], 0.0)
+        one = keep.tile([P, 1], F32, name="one")
+        nc.scalar.activation(one[:], zero[:], ACT.Exp)
+
+        spreads = []
+        for s, col in enumerate((msz_col, size_col)):
+            spread = psum.tile([P, PACK, P], F32, name="spread%d" % s, tag="spread%d" % s)
+            for t in range(PACK):
+                nc.tensor.transpose(spread[:, t, :], col[:, t : t + 1].to_broadcast([P, P]), ident[:])
+            spreads.append(spread)
+
+        q_grouped = keep.tile([P, Q, PACK], BF16, name="q_grouped", align_bytes=64)
+        interleave(nc.scalar.copy, q_grouped[:], q_raw[:])
+        q_codes, q_scales = mx_tiles("q", Q)
+        quantize(nc, q_codes[:], q_scales[:], q_grouped[:])
+
+        wkey_codes, wkey_scales = mx_tiles("wkey", M, "key_bytes")
+        wkey_grouped = keep.tile([P, M, PACK], BF16, name="wkey_grouped", align_bytes=64)
+        split = M // 2
+        interleave(nc.vector.tensor_copy, wkey_grouped[:, :split, :], wkey_raw[:, :, :split])
+        interleave(nc.scalar.copy, wkey_grouped[:, split:, :], wkey_raw[:, :, split:])
+        gate_c = keep.tile([P, 1], F32, name="gate_c")
+        nc.gpsimd.tensor_scalar(gate_c[:], gate[:], GATE_CLAMP, -GATE_CLAMP, ALU.min, ALU.max)
+        gate_exp = keep.tile([P, 2], F32, name="gate_exp", tag="wkey")
+        nc.scalar.activation(gate_exp[:, 0:1], gate_c[:], ACT.Exp, scale=1.0)
+        nc.scalar.activation(gate_exp[:, 1:2], gate_c[:], ACT.Exp, scale=-1.0)
+        gate_inv = keep.tile([P, 2], F32, name="gate_inv")
+        nc.gpsimd.tensor_scalar(gate_inv[:], gate_exp[:], one[:], 1.0, ALU.add, ALU.mult)
+        picked_bytes = keep.tile([P, I], U8, name="picked_bytes", align_bytes=64)
+        nc.vector.tensor_copy(picked_bytes[:], key_bytes[:].indirect(offsets[:]))
+        quantize(nc, wkey_codes[:], wkey_scales[:], wkey_grouped[:])
+        picked_words = keep.tile([P, I], U32, name="picked_words", tag="picked_words", align_bytes=64)
+        nc.vector.tensor_copy(picked_words[:], key_words[:].indirect(offsets[:]))
+
+        def turn(name, rows, grouped):
+            words = rows[:].bitcast(F32)
+            turned = psum.tile([P, 2, P], F32, name=name + "_turned", tag="turned", bufs=4)
+            for u in range(2):
+                nc.tensor.transpose(turned[:, u, :], words[:, u : 2 * P : 2], ident[:])
+            nc.scalar.copy(
+                out=grouped.rearrange("p c t -> p (c t)").bitcast(F32).rearrange("p (c u) -> p c u", u=2),
+                in_=turned[:].rearrange("p u c -> p c u"),
+            )
+
+        denom = keep.tile([P, 2], F32, name="denom")
+        probs = []
+        for s, (key_codes, key_scales) in enumerate(((wkey_codes, wkey_scales), (picked_words, picked_bytes))):
+            scores = psum.tile([P, M], F32, name="scores%d" % s, tag="scores%d" % s)
+            nc.tensor.matmul_mx(
+                out=scores[:], lhsT=q_codes[:].bitcast(FP8X4), lhsT_scale=q_scales[:],
+                rhs=key_codes[:].bitcast(FP8X4), rhs_scale=key_scales[:], start=True, stop=True,
+            )
+            neg_max = keep.tile([P, 1], F32, name="neg_max%d" % s, tag=("keys", "neg_max1")[s])
+            nc.vector.tensor_reduce(neg_max[:], scores[:], mybir.AxisListType.X, ALU.max, negate=True)
+            prob = keep.tile([P, M], F32, name="prob%d" % s, tag="prob%d" % s, align_bytes=64)
+            total = keep.tile([P, 1], F32, name="total%d" % s)
+            nc.scalar.activation(prob[:], scores[:], ACT.Exp, bias=neg_max[:], scale=1.0, accum_out=total[:])
+            nc.scalar.activation(denom[:, s : s + 1], total[:], ACT.Copy, scale=gate_inv[:, s : s + 1])
+            probs.append(prob)
+
+        def pick_values(b, tag, grouped):
+            picked = keep.tile([P, I], BF16, name="picked%d" % b, tag=tag, align_bytes=64)
+            nc.vector.tensor_copy(picked[:], val_raw[b][:].indirect(offsets[:]))
+            turn("val%d" % b, picked, grouped)
+
+        mid_grouped = keep.tile([P, 4 * P, PACK], BF16, name="mid_grouped", tag="mid_grouped", align_bytes=64)
+        pick_values(3, "picked_words", mid_grouped[:, 3 * P :, :])
+        factor = keep.tile([P, 2], F32, name="factor", tag="val3", align_bytes=64)
+        nc.vector.reciprocal(factor[:], denom[:])
+        for s in range(2):
+            rows = keep.tile([P, M], BF16, name="rows%d" % s, align_bytes=64)
+            nc.vector.scalar_tensor_tensor(
+                out=rows[:].rearrange("p (s t) -> p s t", t=PACK),
+                in0=probs[s][:].rearrange("p (s t) -> p s t", t=PACK),
+                scalar=factor[:, s : s + 1],
+                in1=spreads[s][:].rearrange("p t s -> p s t"),
+                op0=ALU.mult, op1=ALU.mult,
+            )
+            turn("rows%d" % s, rows, mid_grouped[:, s * Q : (s + 1) * Q, :])
+        pick_values(2, "prob0", mid_grouped[:, 2 * P : 3 * P, :])
+        grouped1 = keep.tile([P, P, PACK], BF16, name="val_grouped1", align_bytes=64)
+        pick_values(1, "picked1", grouped1[:])
+        mid_codes, mid_scales = mx_tiles("mid", 4 * P, "val1")
+        quantize(nc, mid_codes[:], mid_scales[:], mid_grouped[:])
+        vt = {b: (mid_codes[:, b * P : (b + 1) * P], mid_scales[:, b * P : (b + 1) * P]) for b in (2, 3)}
+        codes, scales = mx_tiles("vt1", P, "mid_grouped")
+        quantize(nc, codes[:], scales[:], grouped1[:])
+        vt[1] = (codes[:], scales[:])
+
+        picked0 = keep.tile([P, I], BF16, name="picked0", align_bytes=64)
+        nc.vector.tensor_copy(picked0[:], val_raw[0][:].indirect(offsets[:]))
+        first = keep.tile([P, 2 * P, PACK], BF16, name="wval_grouped0", tag="val0", align_bytes=64)
+        interleave(nc.scalar.copy, first[:, P:, :], wval_raw[0][:, :, P:])
+        interleave(nc.vector.tensor_copy, first[:, :P, :], wval_raw[0][:, :, :P])
+        grouped0 = keep.tile([P, P, PACK], BF16, name="val_grouped0", tag="wval0", align_bytes=64)
+        turn("val0", picked0, grouped0[:])
+
+        banks = ("scores0", "scores1", "spread0", "spread1")
+        results = [keep.tile([P, 2 * P], F32, name="result%d" % h) for h in range(2)]
+
+        def product(b, codes, scales, copy):
+            acc = psum.tile([P, P], F32, name="acc%d" % b, tag=banks[b])
+            nc.tensor.matmul_mx(
+                out=acc[:], lhsT=mid_codes[:, Q : 2 * Q].bitcast(FP8X4), lhsT_scale=mid_scales[:, Q : 2 * Q],
+                rhs=vt[b][0].bitcast(FP8X4), rhs_scale=vt[b][1], start=True, stop=False,
+            )
+            nc.tensor.matmul_mx(
+                out=acc[:], lhsT=mid_codes[:, :Q].bitcast(FP8X4), lhsT_scale=mid_scales[:, :Q],
+                rhs=codes.bitcast(FP8X4), rhs_scale=scales, start=False, stop=True,
+            )
+            copy(out=results[b // 2][:, (b % 2) * P : (b % 2 + 1) * P], in_=acc[:])
+
+        first_codes, first_scales = mx_tiles("wval_first", 2 * P)
+        quantize(nc, first_codes[:], first_scales[:], first[:])
+        last = []
+        for j, copy in enumerate((nc.vector.tensor_copy, nc.scalar.copy)):
+            g = keep.tile([P, P, PACK], BF16, name="wval_grouped1%d" % j, align_bytes=64)
+            interleave(copy, g[:], wval_raw[1][:, :, j * P : (j + 1) * P])
+            last.append(g)
+        codes, scales = mx_tiles("vt0", P)
+        quantize(nc, codes[:], scales[:], grouped0[:])
+        vt[0] = (codes[:], scales[:])
+        for b, copy in ((1, nc.scalar.copy), (0, nc.vector.tensor_copy)):
+            cols = slice(b * P, (b + 1) * P)
+            product(b, first_codes[:, cols], first_scales[:, cols], copy)
+        nc.sync.dma_start(out=out[:, : 2 * P], in_=results[0][:])
+        for j, copy in enumerate((nc.scalar.copy, nc.vector.tensor_copy)):
+            codes, scales = mx_tiles("wval_last%d" % j, P)
+            quantize(nc, codes[:], scales[:], last[j][:])
+            product(2 + j, codes[:], scales[:], copy)
+        nc.sync.dma_start(out=out[:, 2 * P :], in_=results[1][:])

@@ -20,6 +20,7 @@ P = 128
 PACK = 4
 BLOCKS = E // P
 GATE_CLAMP = 80.0
+WVAL_SPLIT = 192
 
 
 def interleave(copy, dst, src):
@@ -46,8 +47,8 @@ def tile_attend_knn_memory_kernel(tc, query, wkey, wval, keys_words, keys_scales
         ident = keep.tile([P, P], F32, name="ident")
         make_identity(nc, ident[:])
 
-        q_raw = keep.tile([P, PACK, Q], F32, name="q_raw")
-        nc.sync.dma_start(out=q_raw[:], in_=query.rearrange("(p t) c -> p t c", t=PACK))
+        wkey_raw = keep.tile([P, PACK, M], F32, name="wkey_raw")
+        nc.sync.dma_start(out=wkey_raw[:], in_=wkey.rearrange("(p t) c -> p t c", t=PACK))
         offsets = keep.tile([P, I // 16], U16, name="offsets")
         nc.sync.dma_start(offsets[:], offs)
         for quad in range(4):
@@ -55,62 +56,53 @@ def tile_attend_knn_memory_kernel(tc, query, wkey, wval, keys_words, keys_scales
                 out=key_bytes[32 * quad : 32 * quad + 4, :].bitcast(I32),
                 in_=keys_scales[0, 4 * quad : 4 * quad + 4, :].bitcast(I32),
             )
-        wkey_raw = keep.tile([P, PACK, M], F32, name="wkey_raw", tag="wkey")
-        nc.sync.dma_start(out=wkey_raw[:], in_=wkey.rearrange("(p t) c -> p t c", t=PACK))
-        gate = keep.tile([P, 1], F32, name="gate")
-        nc.sync.dma_start(out=gate[:], in_=gb)
-        msz_col = keep.tile([P, PACK], F32, name="msz_col")
-        nc.sync.dma_start(out=msz_col[:], in_=msz.rearrange("o (p t) -> (o p) t", t=PACK))
-        size_col = keep.tile([P, PACK], F32, name="size_col", tag="size_col", align_bytes=64)
-        nc.sync.dma_start(out=size_col[:], in_=size.rearrange("o (p t) -> (o p) t", t=PACK))
+        q_raw = keep.tile([P, PACK, Q], F32, name="q_raw")
+        nc.sync.dma_start(out=q_raw[:], in_=query.rearrange("(p t) c -> p t c", t=PACK))
         key_words = keep.tile([P, T], U32, name="key_words", tag="keys")
         nc.sync.dma_start(
             out=key_words[:].bitcast(I32), in_=keys_words[0].rearrange("p n t -> p (n t)").bitcast(I32)
         )
+        gate = keep.tile([P, 1], F32, name="gate")
+        nc.sync.dma_start(out=gate[:], in_=gb)
+        msz_col = keep.tile([P, PACK], F32, name="msz_col")
+        nc.sync.dma_start(out=msz_col[:], in_=msz.rearrange("o (p t) -> (o p) t", t=PACK))
+        size_col = keep.tile([P, PACK], F32, name="size_col")
+        nc.sync.dma_start(out=size_col[:], in_=size.rearrange("o (p t) -> (o p) t", t=PACK))
         val_raw = {}
         for b in reversed(range(BLOCKS)):
             val_raw[b] = keep.tile([P, T], F32, name="val_raw%d" % b, tag="val%d" % b, align_bytes=64)
             nc.sync.dma_start(out=val_raw[b][:], in_=vals[b * P : (b + 1) * P, :])
-        wval_rows = wval.rearrange("(p t) c -> p t c", t=PACK)
-        wval_raw = {}
-        for h in range(2):
-            wval_raw[h] = keep.tile([P, PACK, 2 * P], F32, name="wval_raw%d" % h, tag="wval%d" % h, align_bytes=64)
-            nc.sync.dma_start(out=wval_raw[h][:], in_=wval_rows[:, :, 2 * P * h : 2 * P * (h + 1)])
+        wval_raw = keep.tile([P, PACK, E], F32, name="wval_raw")
+        nc.sync.dma_start(out=wval_raw[:], in_=wval.rearrange("(p t) c -> p t c", t=PACK))
 
         zero = keep.tile([P, 1], F32, name="zero")
         nc.vector.memset(zero[:], 0.0)
         one = keep.tile([P, 1], F32, name="one")
         nc.scalar.activation(one[:], zero[:], ACT.Exp)
 
-        spreads = []
-        for s, col in enumerate((msz_col, size_col)):
-            spread = psum.tile([P, PACK, P], F32, name="spread%d" % s, tag="spread%d" % s)
-            for t in range(PACK):
-                nc.tensor.transpose(spread[:, t, :], col[:, t : t + 1].to_broadcast([P, P]), ident[:])
-            spreads.append(spread)
-
+        wkey_grouped = keep.tile([P, M, PACK], BF16, name="wkey_grouped", align_bytes=64)
+        split = M // 2
+        interleave(nc.vector.tensor_copy, wkey_grouped[:, :split, :], wkey_raw[:, :, :split])
+        interleave(nc.scalar.copy, wkey_grouped[:, split:, :], wkey_raw[:, :, split:])
+        picked_bytes = keep.tile([P, I], U8, name="picked_bytes", align_bytes=64)
+        nc.vector.tensor_copy(picked_bytes[:], key_bytes[:].indirect(offsets[:]))
+        wkey_codes, wkey_scales = mx_tiles("wkey", M, "key_bytes")
+        quantize(nc, wkey_codes[:], wkey_scales[:], wkey_grouped[:])
         q_grouped = keep.tile([P, Q, PACK], BF16, name="q_grouped", align_bytes=64)
         interleave(nc.scalar.copy, q_grouped[:], q_raw[:])
         q_codes, q_scales = mx_tiles("q", Q)
         quantize(nc, q_codes[:], q_scales[:], q_grouped[:])
 
-        wkey_codes, wkey_scales = mx_tiles("wkey", M, "key_bytes")
-        wkey_grouped = keep.tile([P, M, PACK], BF16, name="wkey_grouped", align_bytes=64)
-        split = M // 2
-        interleave(nc.vector.tensor_copy, wkey_grouped[:, :split, :], wkey_raw[:, :, :split])
-        interleave(nc.scalar.copy, wkey_grouped[:, split:, :], wkey_raw[:, :, split:])
+        picked_words = keep.tile([P, I], U32, name="picked_words", tag="picked_words", align_bytes=64)
+        nc.vector.tensor_copy(picked_words[:], key_words[:].indirect(offsets[:]))
+
         gate_c = keep.tile([P, 1], F32, name="gate_c")
         nc.gpsimd.tensor_scalar(gate_c[:], gate[:], GATE_CLAMP, -GATE_CLAMP, ALU.min, ALU.max)
-        gate_exp = keep.tile([P, 2], F32, name="gate_exp", tag="wkey")
+        gate_exp = keep.tile([P, 2], F32, name="gate_exp")
         nc.scalar.activation(gate_exp[:, 0:1], gate_c[:], ACT.Exp, scale=1.0)
         nc.scalar.activation(gate_exp[:, 1:2], gate_c[:], ACT.Exp, scale=-1.0)
         gate_inv = keep.tile([P, 2], F32, name="gate_inv")
         nc.gpsimd.tensor_scalar(gate_inv[:], gate_exp[:], one[:], 1.0, ALU.add, ALU.mult)
-        picked_bytes = keep.tile([P, I], U8, name="picked_bytes", align_bytes=64)
-        nc.vector.tensor_copy(picked_bytes[:], key_bytes[:].indirect(offsets[:]))
-        quantize(nc, wkey_codes[:], wkey_scales[:], wkey_grouped[:])
-        picked_words = keep.tile([P, I], U32, name="picked_words", tag="picked_words", align_bytes=64)
-        nc.vector.tensor_copy(picked_words[:], key_words[:].indirect(offsets[:]))
 
         def turn(name, rows, grouped):
             words = rows[:].bitcast(F32)
@@ -138,6 +130,13 @@ def tile_attend_knn_memory_kernel(tc, query, wkey, wval, keys_words, keys_scales
             nc.scalar.activation(denom[:, s : s + 1], total[:], ACT.Copy, scale=gate_inv[:, s : s + 1])
             probs.append(prob)
 
+        spreads = []
+        for s, col in enumerate((msz_col, size_col)):
+            spread = psum.tile([P, PACK, P], F32, name="spread%d" % s, tag="scores%d" % s)
+            for t in range(PACK):
+                nc.tensor.transpose(spread[:, t, :], col[:, t : t + 1].to_broadcast([P, P]), ident[:])
+            spreads.append(spread)
+
         def pick_values(b, tag, grouped):
             picked = keep.tile([P, I], BF16, name="picked%d" % b, tag=tag, align_bytes=64)
             nc.vector.tensor_copy(picked[:], val_raw[b][:].indirect(offsets[:]))
@@ -160,52 +159,32 @@ def tile_attend_knn_memory_kernel(tc, query, wkey, wval, keys_words, keys_scales
         pick_values(2, "prob0", mid_grouped[:, 2 * P : 3 * P, :])
         grouped1 = keep.tile([P, P, PACK], BF16, name="val_grouped1", align_bytes=64)
         pick_values(1, "picked1", grouped1[:])
-        mid_codes, mid_scales = mx_tiles("mid", 4 * P, "val1")
+        grouped0 = keep.tile([P, P, PACK], BF16, name="val_grouped0", align_bytes=64)
+        pick_values(0, "picked0", grouped0[:])
+        mid_codes, mid_scales = mx_tiles("mid", 4 * P, "val0")
         quantize(nc, mid_codes[:], mid_scales[:], mid_grouped[:])
-        vt = {b: (mid_codes[:, b * P : (b + 1) * P], mid_scales[:, b * P : (b + 1) * P]) for b in (2, 3)}
-        codes, scales = mx_tiles("vt1", P, "mid_grouped")
-        quantize(nc, codes[:], scales[:], grouped1[:])
-        vt[1] = (codes[:], scales[:])
+        low_codes, low_scales = mx_tiles("low", 2 * P, "picked0")
+        quantize(nc, low_codes[:, P:], low_scales[:, P:], grouped1[:])
+        quantize(nc, low_codes[:, :P], low_scales[:, :P], grouped0[:])
 
-        picked0 = keep.tile([P, I], BF16, name="picked0", align_bytes=64)
-        nc.vector.tensor_copy(picked0[:], val_raw[0][:].indirect(offsets[:]))
-        first = keep.tile([P, 2 * P, PACK], BF16, name="wval_grouped0", tag="val0", align_bytes=64)
-        interleave(nc.scalar.copy, first[:, P:, :], wval_raw[0][:, :, P:])
-        interleave(nc.vector.tensor_copy, first[:, :P, :], wval_raw[0][:, :, :P])
-        grouped0 = keep.tile([P, P, PACK], BF16, name="val_grouped0", tag="wval0", align_bytes=64)
-        turn("val0", picked0, grouped0[:])
-
-        banks = ("scores0", "scores1", "spread0", "spread1")
-        results = [keep.tile([P, 2 * P], F32, name="result%d" % h) for h in range(2)]
-
-        def product(b, codes, scales, copy):
-            acc = psum.tile([P, P], F32, name="acc%d" % b, tag=banks[b])
-            nc.tensor.matmul_mx(
-                out=acc[:], lhsT=mid_codes[:, Q : 2 * Q].bitcast(FP8X4), lhsT_scale=mid_scales[:, Q : 2 * Q],
-                rhs=vt[b][0].bitcast(FP8X4), rhs_scale=vt[b][1], start=True, stop=False,
-            )
-            nc.tensor.matmul_mx(
-                out=acc[:], lhsT=mid_codes[:, :Q].bitcast(FP8X4), lhsT_scale=mid_scales[:, :Q],
-                rhs=codes.bitcast(FP8X4), rhs_scale=scales, start=False, stop=True,
-            )
-            copy(out=results[b // 2][:, (b % 2) * P : (b % 2 + 1) * P], in_=acc[:])
-
-        first_codes, first_scales = mx_tiles("wval_first", 2 * P)
-        quantize(nc, first_codes[:], first_scales[:], first[:])
-        last = []
-        for j, copy in enumerate((nc.vector.tensor_copy, nc.scalar.copy)):
-            g = keep.tile([P, P, PACK], BF16, name="wval_grouped1%d" % j, align_bytes=64)
-            interleave(copy, g[:], wval_raw[1][:, :, j * P : (j + 1) * P])
-            last.append(g)
-        codes, scales = mx_tiles("vt0", P)
-        quantize(nc, codes[:], scales[:], grouped0[:])
-        vt[0] = (codes[:], scales[:])
-        for b, copy in ((1, nc.scalar.copy), (0, nc.vector.tensor_copy)):
-            cols = slice(b * P, (b + 1) * P)
-            product(b, first_codes[:, cols], first_scales[:, cols], copy)
-        nc.sync.dma_start(out=out[:, : 2 * P], in_=results[0][:])
-        for j, copy in enumerate((nc.scalar.copy, nc.vector.tensor_copy)):
-            codes, scales = mx_tiles("wval_last%d" % j, P)
-            quantize(nc, codes[:], scales[:], last[j][:])
-            product(2 + j, codes[:], scales[:], copy)
-        nc.sync.dma_start(out=out[:, 2 * P :], in_=results[1][:])
+        wval_grouped = keep.tile([P, E, PACK], BF16, name="wval_grouped", align_bytes=64)
+        interleave(nc.scalar.copy, wval_grouped[:, :WVAL_SPLIT, :], wval_raw[:, :, :WVAL_SPLIT])
+        interleave(nc.vector.tensor_copy, wval_grouped[:, WVAL_SPLIT:, :], wval_raw[:, :, WVAL_SPLIT:])
+        banks = ("scores0", "scores1", "sums2", "sums3")
+        for h, (val_codes, val_scales) in ((1, (mid_codes[:, 2 * P :], mid_scales[:, 2 * P :])), (0, (low_codes[:], low_scales[:]))):
+            codes, scales = mx_tiles("wval%d" % h, 2 * P)
+            quantize(nc, codes[:], scales[:], wval_grouped[:, 2 * P * h : 2 * P * (h + 1), :])
+            result = keep.tile([P, 2 * P], F32, name="result%d" % h)
+            for j, copy in enumerate((nc.scalar.copy, nc.vector.tensor_copy)):
+                cols = slice(j * P, (j + 1) * P)
+                acc = psum.tile([P, P], F32, name="acc%d%d" % (h, j), tag=banks[2 * h + j])
+                nc.tensor.matmul_mx(
+                    out=acc[:], lhsT=mid_codes[:, Q : 2 * Q].bitcast(FP8X4), lhsT_scale=mid_scales[:, Q : 2 * Q],
+                    rhs=val_codes[:, cols].bitcast(FP8X4), rhs_scale=val_scales[:, cols], start=True, stop=False,
+                )
+                nc.tensor.matmul_mx(
+                    out=acc[:], lhsT=mid_codes[:, :Q].bitcast(FP8X4), lhsT_scale=mid_scales[:, :Q],
+                    rhs=codes[:, cols].bitcast(FP8X4), rhs_scale=scales[:, cols], start=False, stop=True,
+                )
+                copy(out=result[:, cols], in_=acc[:])
+            nc.sync.dma_start(out=out[:, 2 * P * h : 2 * P * (h + 1)], in_=result[:])

@@ -19,7 +19,6 @@ ACT = mybir.ActivationFunctionType
 P = 128
 PACK = 4
 BLOCKS = E // P
-GATE_CLAMP = 80.0
 WVAL_SPLIT = 192
 
 
@@ -42,6 +41,8 @@ def tile_attend_knn_memory_kernel(tc, query, wkey, wval, keys_words, keys_scales
             scales = keep.tile([P, width], U8, name=name + "_scales", tag=scale_tag or name + "_scales", align_bytes=64)
             return codes, scales
 
+        vectors = keep.tile([P, P], F32, name="vectors")
+        nc.gpsimd.memset(vectors[:], 0.0)
         key_bytes = keep.tile([P, T], U8, name="key_bytes", tag="key_bytes", align_bytes=64)
         nc.gpsimd.memset(key_bytes[:].bitcast(I32), 0)
         ident = keep.tile([P, P], F32, name="ident")
@@ -51,10 +52,10 @@ def tile_attend_knn_memory_kernel(tc, query, wkey, wval, keys_words, keys_scales
         nc.sync.dma_start(out=wkey_raw[:], in_=wkey.rearrange("(p t) c -> p t c", t=PACK))
         offsets = keep.tile([P, I // 16], U16, name="offsets")
         nc.sync.dma_start(offsets[:], offs)
-        for quad in range(4):
+        for row in range(4):
             nc.sync.dma_start(
-                out=key_bytes[32 * quad : 32 * quad + 4, :].bitcast(I32),
-                in_=keys_scales[0, 4 * quad : 4 * quad + 4, :].bitcast(I32),
+                out=key_bytes[row:P:32, :].bitcast(I32),
+                in_=keys_scales[0, row:16:4, :].bitcast(I32),
             )
         q_raw = keep.tile([P, PACK, Q], F32, name="q_raw")
         nc.sync.dma_start(out=q_raw[:], in_=query.rearrange("(p t) c -> p t c", t=PACK))
@@ -62,12 +63,9 @@ def tile_attend_knn_memory_kernel(tc, query, wkey, wval, keys_words, keys_scales
         nc.sync.dma_start(
             out=key_words[:].bitcast(I32), in_=keys_words[0].rearrange("p n t -> p (n t)").bitcast(I32)
         )
-        gate = keep.tile([P, 1], F32, name="gate")
-        nc.sync.dma_start(out=gate[:], in_=gb)
-        msz_col = keep.tile([P, PACK], F32, name="msz_col")
-        nc.sync.dma_start(out=msz_col[:], in_=msz.rearrange("o (p t) -> (o p) t", t=PACK))
-        size_col = keep.tile([P, PACK], F32, name="size_col")
-        nc.sync.dma_start(out=size_col[:], in_=size.rearrange("o (p t) -> (o p) t", t=PACK))
+        nc.sync.dma_start(out=vectors[0:1, :], in_=gb.rearrange("q o -> o q"))
+        nc.sync.dma_start(out=vectors[4:8, :], in_=msz.rearrange("o (b c) -> (o b) c", c=P))
+        nc.sync.dma_start(out=vectors[8:12, :], in_=size.rearrange("o (b c) -> (o b) c", c=P))
         val_raw = {}
         for b in reversed(range(BLOCKS)):
             val_raw[b] = keep.tile([P, T], F32, name="val_raw%d" % b, tag="val%d" % b, align_bytes=64)
@@ -96,13 +94,15 @@ def tile_attend_knn_memory_kernel(tc, query, wkey, wval, keys_words, keys_scales
         picked_words = keep.tile([P, I], U32, name="picked_words", tag="picked_words", align_bytes=64)
         nc.vector.tensor_copy(picked_words[:], key_words[:].indirect(offsets[:]))
 
-        gate_c = keep.tile([P, 1], F32, name="gate_c")
-        nc.gpsimd.tensor_scalar(gate_c[:], gate[:], GATE_CLAMP, -GATE_CLAMP, ALU.min, ALU.max)
+        vectors_turned = psum.tile([P, P], F32, name="vectors_turned", tag="scores1")
+        nc.tensor.transpose(vectors_turned[:], vectors[:], ident[:])
+        gate = keep.tile([P, 1], F32, name="gate", tag="total0")
+        nc.scalar.copy(out=gate[:], in_=vectors_turned[:, 0:1])
+        columns = keep.tile([P, 8], F32, name="columns")
+        nc.scalar.copy(out=columns[:], in_=vectors_turned[:, 4:12])
         gate_exp = keep.tile([P, 2], F32, name="gate_exp")
-        nc.scalar.activation(gate_exp[:, 0:1], gate_c[:], ACT.Exp, scale=1.0)
-        nc.scalar.activation(gate_exp[:, 1:2], gate_c[:], ACT.Exp, scale=-1.0)
-        gate_inv = keep.tile([P, 2], F32, name="gate_inv")
-        nc.gpsimd.tensor_scalar(gate_inv[:], gate_exp[:], one[:], 1.0, ALU.add, ALU.mult)
+        nc.scalar.activation(gate_exp[:, 0:1], gate[:], ACT.Exp, scale=one[:])
+        nc.scalar.activation(gate_exp[:, 1:2], gate[:], ACT.Exp, scale=-1.0)
 
         def turn(name, rows, grouped):
             words = rows[:].bitcast(F32)
@@ -125,16 +125,16 @@ def tile_attend_knn_memory_kernel(tc, query, wkey, wval, keys_words, keys_scales
             neg_max = keep.tile([P, 1], F32, name="neg_max%d" % s, tag=("keys", "neg_max1")[s])
             nc.vector.tensor_reduce(neg_max[:], scores[:], mybir.AxisListType.X, ALU.max, negate=True)
             prob = keep.tile([P, M], F32, name="prob%d" % s, tag="prob%d" % s, align_bytes=64)
-            total = keep.tile([P, 1], F32, name="total%d" % s)
+            total = keep.tile([P, 1], F32, name="total%d" % s, tag="total%d" % s)
             nc.scalar.activation(prob[:], scores[:], ACT.Exp, bias=neg_max[:], scale=1.0, accum_out=total[:])
-            nc.scalar.activation(denom[:, s : s + 1], total[:], ACT.Copy, scale=gate_inv[:, s : s + 1])
+            nc.scalar.activation(denom[:, s : s + 1], total[:], ACT.Identity, scale=gate_exp[:, s : s + 1], bias=total[:])
             probs.append(prob)
 
         spreads = []
-        for s, col in enumerate((msz_col, size_col)):
+        for s in range(2):
             spread = psum.tile([P, PACK, P], F32, name="spread%d" % s, tag="scores%d" % s)
             for t in range(PACK):
-                nc.tensor.transpose(spread[:, t, :], col[:, t : t + 1].to_broadcast([P, P]), ident[:])
+                nc.tensor.transpose(spread[:, t, :], columns[:, 4 * s + t : 4 * s + t + 1].to_broadcast([P, P]), ident[:])
             spreads.append(spread)
 
         def pick_values(b, tag, grouped):
@@ -149,10 +149,10 @@ def tile_attend_knn_memory_kernel(tc, query, wkey, wval, keys_words, keys_scales
         for s in range(2):
             rows = keep.tile([P, M], BF16, name="rows%d" % s, align_bytes=64)
             nc.vector.scalar_tensor_tensor(
-                out=rows[:].rearrange("p (s t) -> p s t", t=PACK),
-                in0=probs[s][:].rearrange("p (s t) -> p s t", t=PACK),
+                out=rows[:],
+                in0=probs[s][:],
                 scalar=factor[:, s : s + 1],
-                in1=spreads[s][:].rearrange("p t s -> p s t"),
+                in1=spreads[s][:].rearrange("p b c -> p (b c)"),
                 op0=ALU.mult, op1=ALU.mult,
             )
             turn("rows%d" % s, rows, mid_grouped[:, s * Q : (s + 1) * Q, :])

@@ -19,7 +19,7 @@ ACT = mybir.ActivationFunctionType
 P = 128
 PACK = 4
 BLOCKS = E // P
-WVAL_SPLIT = 192
+WVAL_SPLIT = 224
 
 
 def interleave(copy, dst, src):
@@ -79,10 +79,10 @@ def tile_attend_knn_memory_kernel(tc, query, wkey, wval, keys_words, keys_scales
         nc.scalar.activation(one[:], zero[:], ACT.Exp)
 
         wkey_grouped = keep.tile([P, M, PACK], BF16, name="wkey_grouped", align_bytes=64)
-        split = M // 2
+        split = 192
         interleave(nc.vector.tensor_copy, wkey_grouped[:, :split, :], wkey_raw[:, :, :split])
         interleave(nc.scalar.copy, wkey_grouped[:, split:, :], wkey_raw[:, :, split:])
-        picked_bytes = keep.tile([P, I], U8, name="picked_bytes", align_bytes=64)
+        picked_bytes = keep.tile([P, I], U8, name="picked_bytes", tag="picked_bytes", align_bytes=64)
         nc.vector.tensor_copy(picked_bytes[:], key_bytes[:].indirect(offsets[:]))
         wkey_codes, wkey_scales = mx_tiles("wkey", M, "key_bytes")
         quantize(nc, wkey_codes[:], wkey_scales[:], wkey_grouped[:])
@@ -98,8 +98,8 @@ def tile_attend_knn_memory_kernel(tc, query, wkey, wval, keys_words, keys_scales
         nc.tensor.transpose(vectors_turned[:], vectors[:], ident[:])
         gate = keep.tile([P, 1], F32, name="gate", tag="total0")
         nc.scalar.copy(out=gate[:], in_=vectors_turned[:, 0:1])
-        columns = keep.tile([P, 8], F32, name="columns")
-        nc.scalar.copy(out=columns[:], in_=vectors_turned[:, 4:12])
+        weight_cols = keep.tile([P, 8], F32, name="weight_cols")
+        nc.scalar.copy(out=weight_cols[:], in_=vectors_turned[:, 4:12])
         gate_exp = keep.tile([P, 2], F32, name="gate_exp")
         nc.scalar.activation(gate_exp[:, 0:1], gate[:], ACT.Exp, scale=one[:])
         nc.scalar.activation(gate_exp[:, 1:2], gate[:], ACT.Exp, scale=-1.0)
@@ -130,9 +130,11 @@ def tile_attend_knn_memory_kernel(tc, query, wkey, wval, keys_words, keys_scales
             nc.scalar.activation(denom[:, s : s + 1], total[:], ACT.Identity, scale=gate_exp[:, s : s + 1], bias=total[:])
             probs.append(prob)
 
+        columns = keep.tile([P, 8], F32, name="columns", tag="picked_bytes", align_bytes=64)
+        nc.gpsimd.tensor_copy(columns[:], weight_cols[:])
         spreads = []
         for s in range(2):
-            spread = psum.tile([P, PACK, P], F32, name="spread%d" % s, tag="scores%d" % s)
+            spread = psum.tile([P, PACK, P], F32, name="spread%d" % s, tag="sums%d" % (2 + s))
             for t in range(PACK):
                 nc.tensor.transpose(spread[:, t, :], columns[:, 4 * s + t : 4 * s + t + 1].to_broadcast([P, P]), ident[:])
             spreads.append(spread)

@@ -19,7 +19,7 @@ ACT = mybir.ActivationFunctionType
 P = 128
 PACK = 4
 BLOCKS = E // P
-WVAL_SPLIT = 224
+SHARE = 288
 
 
 def interleave(copy, dst, src):
@@ -44,7 +44,7 @@ def tile_attend_knn_memory_kernel(tc, query, wkey, wval, keys_words, keys_scales
         vectors = keep.tile([P, P], F32, name="vectors")
         nc.gpsimd.memset(vectors[:], 0.0)
         key_bytes = keep.tile([P, T], U8, name="key_bytes", tag="key_bytes", align_bytes=64)
-        nc.gpsimd.memset(key_bytes[:].bitcast(I32), 0)
+        nc.vector.memset(key_bytes[:].bitcast(I32), 0)
         ident = keep.tile([P, P], F32, name="ident")
         make_identity(nc, ident[:])
 
@@ -67,11 +67,15 @@ def tile_attend_knn_memory_kernel(tc, query, wkey, wval, keys_words, keys_scales
         nc.sync.dma_start(out=vectors[4:8, :], in_=msz.rearrange("o (b c) -> (o b) c", c=P))
         nc.sync.dma_start(out=vectors[8:12, :], in_=size.rearrange("o (b c) -> (o b) c", c=P))
         val_raw = {}
-        for b in reversed(range(BLOCKS)):
+        for b in range(BLOCKS):
             val_raw[b] = keep.tile([P, T], F32, name="val_raw%d" % b, tag="val%d" % b, align_bytes=64)
             nc.sync.dma_start(out=val_raw[b][:], in_=vals[b * P : (b + 1) * P, :])
-        wval_raw = keep.tile([P, PACK, E], F32, name="wval_raw")
-        nc.sync.dma_start(out=wval_raw[:], in_=wval.rearrange("(p t) c -> p t c", t=PACK))
+        wval_rows = wval.rearrange("(p t) c -> p t c", t=PACK)
+        wval_raw = []
+        for b in range(BLOCKS):
+            piece = keep.tile([P, PACK, P], F32, name="wval_raw%d" % b, tag="wval_raw%d" % b, align_bytes=64)
+            nc.sync.dma_start(out=piece[:], in_=wval_rows[:, :, b * P : (b + 1) * P])
+            wval_raw.append(piece)
 
         zero = keep.tile([P, 1], F32, name="zero")
         nc.vector.memset(zero[:], 0.0)
@@ -86,11 +90,11 @@ def tile_attend_knn_memory_kernel(tc, query, wkey, wval, keys_words, keys_scales
         nc.vector.tensor_copy(picked_bytes[:], key_bytes[:].indirect(offsets[:]))
         wkey_codes, wkey_scales = mx_tiles("wkey", M, "key_bytes")
         quantize(nc, wkey_codes[:], wkey_scales[:], wkey_grouped[:])
+
         q_grouped = keep.tile([P, Q, PACK], BF16, name="q_grouped", align_bytes=64)
         interleave(nc.scalar.copy, q_grouped[:], q_raw[:])
         q_codes, q_scales = mx_tiles("q", Q)
         quantize(nc, q_codes[:], q_scales[:], q_grouped[:])
-
         picked_words = keep.tile([P, I], U32, name="picked_words", tag="picked_words", align_bytes=64)
         nc.vector.tensor_copy(picked_words[:], key_words[:].indirect(offsets[:]))
 
@@ -98,15 +102,15 @@ def tile_attend_knn_memory_kernel(tc, query, wkey, wval, keys_words, keys_scales
         nc.tensor.transpose(vectors_turned[:], vectors[:], ident[:])
         gate = keep.tile([P, 1], F32, name="gate", tag="total0")
         nc.scalar.copy(out=gate[:], in_=vectors_turned[:, 0:1])
-        weight_cols = keep.tile([P, 8], F32, name="weight_cols")
-        nc.scalar.copy(out=weight_cols[:], in_=vectors_turned[:, 4:12])
+        columns = keep.tile([P, 8], F32, name="columns")
+        nc.scalar.copy(out=columns[:], in_=vectors_turned[:, 4:12])
         gate_exp = keep.tile([P, 2], F32, name="gate_exp")
         nc.scalar.activation(gate_exp[:, 0:1], gate[:], ACT.Exp, scale=one[:])
         nc.scalar.activation(gate_exp[:, 1:2], gate[:], ACT.Exp, scale=-1.0)
 
-        def turn(name, rows, grouped):
+        def turn(name, rows, grouped, bank="turned", bufs=3):
             words = rows[:].bitcast(F32)
-            turned = psum.tile([P, 2, P], F32, name=name + "_turned", tag="turned", bufs=4)
+            turned = psum.tile([P, 2, P], F32, name=name + "_turned", tag=bank, bufs=bufs)
             for u in range(2):
                 nc.tensor.transpose(turned[:, u, :], words[:, u : 2 * P : 2], ident[:])
             nc.scalar.copy(
@@ -130,8 +134,6 @@ def tile_attend_knn_memory_kernel(tc, query, wkey, wval, keys_words, keys_scales
             nc.scalar.activation(denom[:, s : s + 1], total[:], ACT.Identity, scale=gate_exp[:, s : s + 1], bias=total[:])
             probs.append(prob)
 
-        columns = keep.tile([P, 8], F32, name="columns", tag="picked_bytes", align_bytes=64)
-        nc.gpsimd.tensor_copy(columns[:], weight_cols[:])
         spreads = []
         for s in range(2):
             spread = psum.tile([P, PACK, P], F32, name="spread%d" % s, tag="sums%d" % (2 + s))
@@ -139,14 +141,29 @@ def tile_attend_knn_memory_kernel(tc, query, wkey, wval, keys_words, keys_scales
                 nc.tensor.transpose(spread[:, t, :], columns[:, 4 * s + t : 4 * s + t + 1].to_broadcast([P, P]), ident[:])
             spreads.append(spread)
 
-        def pick_values(b, tag, grouped):
-            picked = keep.tile([P, I], BF16, name="picked%d" % b, tag=tag, align_bytes=64)
-            nc.vector.tensor_copy(picked[:], val_raw[b][:].indirect(offsets[:]))
-            turn("val%d" % b, picked, grouped)
+        def pick_values(b, vector_slots):
+            picked = keep.tile([P, I], BF16, name="picked%d" % b, align_bytes=64)
+            cut = vector_slots // 16
+            if vector_slots > 0:
+                nc.vector.tensor_copy(picked[:, :vector_slots], val_raw[b][:].indirect(offsets[:, :cut]))
+            if vector_slots < I:
+                nc.scalar.activation(picked[:, vector_slots:], val_raw[b][:].indirect(offsets[:, cut:]), ACT.Copy)
+            return picked
 
-        mid_grouped = keep.tile([P, 4 * P, PACK], BF16, name="mid_grouped", tag="mid_grouped", align_bytes=64)
-        pick_values(3, "picked_words", mid_grouped[:, 3 * P :, :])
-        factor = keep.tile([P, 2], F32, name="factor", tag="val3", align_bytes=64)
+        def grouped_tile(name, width, tag=None):
+            return keep.tile([P, width, PACK], BF16, name=name, tag=tag or name, align_bytes=64)
+
+        def quantized(name, grouped, tag=None):
+            codes, scales = mx_tiles(name, grouped.shape[1], tag)
+            quantize(nc, codes[:], scales[:], grouped)
+            return codes, scales
+
+        val_mx = {}
+        picked0 = pick_values(0, I)
+        picked1 = pick_values(1, 0)
+        mid_grouped = grouped_tile("mid_grouped", 4 * P, "val1")
+        turn("val0", picked0, mid_grouped[:, 2 * P : 3 * P, :])
+        factor = keep.tile([P, 2], F32, name="factor", tag="val0", align_bytes=64)
         nc.vector.reciprocal(factor[:], denom[:])
         for s in range(2):
             rows = keep.tile([P, M], BF16, name="rows%d" % s, align_bytes=64)
@@ -158,35 +175,44 @@ def tile_attend_knn_memory_kernel(tc, query, wkey, wval, keys_words, keys_scales
                 op0=ALU.mult, op1=ALU.mult,
             )
             turn("rows%d" % s, rows, mid_grouped[:, s * Q : (s + 1) * Q, :])
-        pick_values(2, "prob0", mid_grouped[:, 2 * P : 3 * P, :])
-        grouped1 = keep.tile([P, P, PACK], BF16, name="val_grouped1", align_bytes=64)
-        pick_values(1, "picked1", grouped1[:])
-        grouped0 = keep.tile([P, P, PACK], BF16, name="val_grouped0", align_bytes=64)
-        pick_values(0, "picked0", grouped0[:])
-        mid_codes, mid_scales = mx_tiles("mid", 4 * P, "val0")
-        quantize(nc, mid_codes[:], mid_scales[:], mid_grouped[:])
-        low_codes, low_scales = mx_tiles("low", 2 * P, "picked0")
-        quantize(nc, low_codes[:, P:], low_scales[:, P:], grouped1[:])
-        quantize(nc, low_codes[:, :P], low_scales[:, :P], grouped0[:])
+        turn("val1", picked1, mid_grouped[:, 3 * P :, :])
+        pair_grouped = grouped_tile("pair_grouped", 2 * P)
+        turn("val2", pick_values(2, I), pair_grouped[:, :P, :])
+        mid_codes, mid_scales = quantized("mid", mid_grouped[:], "val2")
+        for b in range(2):
+            cols = slice((b + 2) * P, (b + 3) * P)
+            val_mx[b] = (mid_codes[:, cols], mid_scales[:, cols])
+        picked3 = pick_values(3, SHARE)
 
-        wval_grouped = keep.tile([P, E, PACK], BF16, name="wval_grouped", align_bytes=64)
-        interleave(nc.scalar.copy, wval_grouped[:, :WVAL_SPLIT, :], wval_raw[:, :, :WVAL_SPLIT])
-        interleave(nc.vector.tensor_copy, wval_grouped[:, WVAL_SPLIT:, :], wval_raw[:, :, WVAL_SPLIT:])
-        banks = ("scores0", "scores1", "sums2", "sums3")
-        for h, (val_codes, val_scales) in ((1, (mid_codes[:, 2 * P :], mid_scales[:, 2 * P :])), (0, (low_codes[:], low_scales[:]))):
-            codes, scales = mx_tiles("wval%d" % h, 2 * P)
-            quantize(nc, codes[:], scales[:], wval_grouped[:, 2 * P * h : 2 * P * (h + 1), :])
-            result = keep.tile([P, 2 * P], F32, name="result%d" % h)
-            for j, copy in enumerate((nc.scalar.copy, nc.vector.tensor_copy)):
-                cols = slice(j * P, (j + 1) * P)
-                acc = psum.tile([P, P], F32, name="acc%d%d" % (h, j), tag=banks[2 * h + j])
+        wval_mx = {}
+        interleave(nc.vector.tensor_copy, pair_grouped[:, P:, :], wval_raw[0][:])
+        pair_codes, pair_scales = quantized("pair", pair_grouped[:])
+        val_mx[2] = (pair_codes[:, :P], pair_scales[:, :P])
+        wval_mx[0] = (pair_codes[:, P:], pair_scales[:, P:])
+        wval_grouped = {b: grouped_tile("wval_grouped%d" % b, P) for b in (1, 2, 3)}
+        interleave(nc.scalar.copy, wval_grouped[1][:], wval_raw[1][:])
+        grouped3 = grouped_tile("val_grouped3", P, "pair_grouped")
+        turn("val3", picked3, grouped3[:], "last_turned", 1)
+        interleave(nc.vector.tensor_copy, wval_grouped[2][:], wval_raw[2][:])
+        interleave(nc.scalar.copy, wval_grouped[3][:], wval_raw[3][:])
+        for b in (1, 2):
+            wval_mx[b] = quantized("wval%d" % b, wval_grouped[b][:])
+        val_mx[3] = quantized("val3", grouped3[:])
+        wval_mx[3] = quantized("wval3", wval_grouped[3][:])
+
+        window_weights = (mid_codes[:, :Q], mid_scales[:, :Q])
+        memory_weights = (mid_codes[:, Q : 2 * Q], mid_scales[:, Q : 2 * Q])
+        banks = ("last_turned", "scores1", "sums2", "sums3")
+        result = keep.tile([P, E], F32, name="result")
+        for b in range(BLOCKS):
+            cols = slice(b * P, (b + 1) * P)
+            acc = psum.tile([P, P], F32, name="acc%d" % b, tag=banks[b])
+            passes = [(memory_weights, val_mx[b]), (window_weights, wval_mx[b])]
+            for n, ((w_codes, w_scales), (v_codes, v_scales)) in enumerate(passes):
                 nc.tensor.matmul_mx(
-                    out=acc[:], lhsT=mid_codes[:, Q : 2 * Q].bitcast(FP8X4), lhsT_scale=mid_scales[:, Q : 2 * Q],
-                    rhs=val_codes[:, cols].bitcast(FP8X4), rhs_scale=val_scales[:, cols], start=True, stop=False,
+                    out=acc[:], lhsT=w_codes.bitcast(FP8X4), lhsT_scale=w_scales,
+                    rhs=v_codes[:].bitcast(FP8X4), rhs_scale=v_scales[:], start=n == 0, stop=n == 1,
                 )
-                nc.tensor.matmul_mx(
-                    out=acc[:], lhsT=mid_codes[:, :Q].bitcast(FP8X4), lhsT_scale=mid_scales[:, :Q],
-                    rhs=codes[:, cols].bitcast(FP8X4), rhs_scale=scales[:, cols], start=False, stop=True,
-                )
-                copy(out=result[:, cols], in_=acc[:])
-            nc.sync.dma_start(out=out[:, 2 * P * h : 2 * P * (h + 1)], in_=result[:])
+            (nc.vector.tensor_copy if b == 3 else nc.scalar.copy)(out=result[:, cols], in_=acc[:])
+            if b % 2 == 1:
+                nc.sync.dma_start(out=out[:, (b - 1) * P : (b + 1) * P], in_=result[:, (b - 1) * P : (b + 1) * P])

@@ -19,7 +19,7 @@ ACT = mybir.ActivationFunctionType
 P = 128
 PACK = 4
 BLOCKS = E // P
-SHARE = 288
+SHARE = 352
 
 
 def interleave(copy, dst, src):
@@ -72,10 +72,10 @@ def tile_attend_knn_memory_kernel(tc, query, wkey, wval, keys_words, keys_scales
             nc.sync.dma_start(out=val_raw[b][:], in_=vals[b * P : (b + 1) * P, :])
         wval_rows = wval.rearrange("(p t) c -> p t c", t=PACK)
         wval_raw = []
-        for b in range(BLOCKS):
-            piece = keep.tile([P, PACK, P], F32, name="wval_raw%d" % b, tag="wval_raw%d" % b, align_bytes=64)
-            nc.sync.dma_start(out=piece[:], in_=wval_rows[:, :, b * P : (b + 1) * P])
-            wval_raw.append(piece)
+        for first, last in ((0, 2), (2, 3), (3, 4)):
+            piece = keep.tile([P, PACK, (last - first) * P], F32, name="wval_raw%d" % first, tag="wval_raw%d" % first, align_bytes=64)
+            nc.sync.dma_start(out=piece[:], in_=wval_rows[:, :, first * P : last * P])
+            wval_raw.extend(piece[:, :, b * P : (b + 1) * P] for b in range(last - first))
 
         zero = keep.tile([P, 1], F32, name="zero")
         nc.vector.memset(zero[:], 0.0)
@@ -102,8 +102,8 @@ def tile_attend_knn_memory_kernel(tc, query, wkey, wval, keys_words, keys_scales
         nc.tensor.transpose(vectors_turned[:], vectors[:], ident[:])
         gate = keep.tile([P, 1], F32, name="gate", tag="total0")
         nc.scalar.copy(out=gate[:], in_=vectors_turned[:, 0:1])
-        columns = keep.tile([P, 8], F32, name="columns")
-        nc.scalar.copy(out=columns[:], in_=vectors_turned[:, 4:12])
+        weight_cols = keep.tile([P, 8], F32, name="weight_cols")
+        nc.scalar.copy(out=weight_cols[:], in_=vectors_turned[:, 4:12])
         gate_exp = keep.tile([P, 2], F32, name="gate_exp")
         nc.scalar.activation(gate_exp[:, 0:1], gate[:], ACT.Exp, scale=one[:])
         nc.scalar.activation(gate_exp[:, 1:2], gate[:], ACT.Exp, scale=-1.0)
@@ -134,6 +134,7 @@ def tile_attend_knn_memory_kernel(tc, query, wkey, wval, keys_words, keys_scales
             nc.scalar.activation(denom[:, s : s + 1], total[:], ACT.Identity, scale=gate_exp[:, s : s + 1], bias=total[:])
             probs.append(prob)
 
+        columns = weight_cols
         spreads = []
         for s in range(2):
             spread = psum.tile([P, PACK, P], F32, name="spread%d" % s, tag="sums%d" % (2 + s))
@@ -163,7 +164,7 @@ def tile_attend_knn_memory_kernel(tc, query, wkey, wval, keys_words, keys_scales
         picked1 = pick_values(1, 0)
         mid_grouped = grouped_tile("mid_grouped", 4 * P, "val1")
         turn("val0", picked0, mid_grouped[:, 2 * P : 3 * P, :])
-        factor = keep.tile([P, 2], F32, name="factor", tag="val0", align_bytes=64)
+        factor = keep.tile([P, 2], F32, name="factor")
         nc.vector.reciprocal(factor[:], denom[:])
         for s in range(2):
             rows = keep.tile([P, M], BF16, name="rows%d" % s, align_bytes=64)
@@ -191,7 +192,7 @@ def tile_attend_knn_memory_kernel(tc, query, wkey, wval, keys_words, keys_scales
         wval_mx[0] = (pair_codes[:, P:], pair_scales[:, P:])
         wval_grouped = {b: grouped_tile("wval_grouped%d" % b, P) for b in (1, 2, 3)}
         interleave(nc.scalar.copy, wval_grouped[1][:], wval_raw[1][:])
-        grouped3 = grouped_tile("val_grouped3", P, "pair_grouped")
+        grouped3 = grouped_tile("val_grouped3", P, "wval_raw0")
         turn("val3", picked3, grouped3[:], "last_turned", 1)
         interleave(nc.vector.tensor_copy, wval_grouped[2][:], wval_raw[2][:])
         interleave(nc.scalar.copy, wval_grouped[3][:], wval_raw[3][:])
@@ -214,5 +215,6 @@ def tile_attend_knn_memory_kernel(tc, query, wkey, wval, keys_words, keys_scales
                     rhs=v_codes[:].bitcast(FP8X4), rhs_scale=v_scales[:], start=n == 0, stop=n == 1,
                 )
             (nc.vector.tensor_copy if b == 3 else nc.scalar.copy)(out=result[:, cols], in_=acc[:])
-            if b % 2 == 1:
-                nc.sync.dma_start(out=out[:, (b - 1) * P : (b + 1) * P], in_=result[:, (b - 1) * P : (b + 1) * P])
+            if b > 0:
+                stored = slice(0 if b == 1 else b * P, (b + 1) * P)
+                nc.sync.dma_start(out=out[:, stored], in_=result[:, stored])

@@ -19,15 +19,13 @@ ACT = mybir.ActivationFunctionType
 P = 128
 PACK = 4
 BLOCKS = E // P
-SHARE = 352
+WKEY_VECTOR_COLUMNS = 288
+LAST_GATHER_VECTOR_SLOTS = 320
+WVAL2_SCALAR_COLUMNS = 64
 
 
 def interleave(copy, dst, src):
     copy(out=dst.rearrange("p (c i) t -> p c t i", i=4), in_=src.rearrange("p t (c i) -> p c t i", i=4))
-
-
-def quantize(nc, codes, scales, grouped):
-    nc.vector.quantize_mx(out=codes.bitcast(FP8X4), scales=scales, in_=grouped.rearrange("p c t -> p (c t)"))
 
 
 def tile_attend_knn_memory_kernel(tc, query, wkey, wval, keys_words, keys_scales, vals, gb, msz, size, offs, out):
@@ -36,81 +34,106 @@ def tile_attend_knn_memory_kernel(tc, query, wkey, wval, keys_words, keys_scales
         keep = ctx.enter_context(tc.tile_pool(name="keep", bufs=1))
         psum = ctx.enter_context(tc.psum_pool(name="psum", bufs=1))
 
-        def mx_tiles(name, width, tag=None, scale_tag=None):
-            codes = keep.tile([P, width], U32, name=name + "_codes", tag=tag or name + "_codes", align_bytes=64)
-            scales = keep.tile([P, width], U8, name=name + "_scales", tag=scale_tag or name + "_scales", align_bytes=64)
-            return codes, scales
+        def sbuf(name, shape, dtype, reuse=None):
+            return keep.tile(shape, dtype, name=name, tag=reuse or name, align_bytes=64)
 
-        vectors = keep.tile([P, P], F32, name="vectors")
-        nc.gpsimd.memset(vectors[:], 0.0)
-        key_bytes = keep.tile([P, T], U8, name="key_bytes", tag="key_bytes", align_bytes=64)
-        nc.vector.memset(key_bytes[:].bitcast(I32), 0)
-        ident = keep.tile([P, P], F32, name="ident")
+        def quantized(name, grouped, reuse=None):
+            width = grouped.shape[1]
+            codes = sbuf(name + "_codes", [P, width], U32, reuse)
+            scales = sbuf(name + "_scales", [P, width], U8)
+            nc.vector.quantize_mx(out=codes[:].bitcast(FP8X4), scales=scales[:], in_=grouped.rearrange("p c t -> p (c t)"))
+            return codes[:], scales[:]
+
+        def columns_of(operand, first, width=P):
+            return operand[0][:, first : first + width], operand[1][:, first : first + width]
+
+        def product(acc, stationary, moving, start, stop):
+            nc.tensor.matmul_mx(
+                out=acc, lhsT=stationary[0].bitcast(FP8X4), lhsT_scale=stationary[1],
+                rhs=moving[0].bitcast(FP8X4), rhs_scale=moving[1], start=start, stop=stop,
+            )
+
+        key_bytes = sbuf("key_bytes", [P, T], U8)
+        nc.gpsimd.memset(key_bytes[:].bitcast(I32), 0)
+        vectors = sbuf("vectors", [P, P], F32)
+        nc.vector.memset(vectors[:], 0.0)
+        ident = sbuf("ident", [P, P], F32)
         make_identity(nc, ident[:])
 
-        wkey_raw = keep.tile([P, PACK, M], F32, name="wkey_raw")
-        nc.sync.dma_start(out=wkey_raw[:], in_=wkey.rearrange("(p t) c -> p t c", t=PACK))
+        q_raw = sbuf("q_raw", [P, PACK, Q], F32)
+        nc.sync.dma_start(out=q_raw[:], in_=query.rearrange("(p t) c -> p t c", t=PACK))
         offsets = keep.tile([P, I // 16], U16, name="offsets")
         nc.sync.dma_start(offsets[:], offs)
-        for row in range(4):
-            nc.sync.dma_start(
-                out=key_bytes[row:P:32, :].bitcast(I32),
-                in_=keys_scales[0, row:16:4, :].bitcast(I32),
-            )
-        q_raw = keep.tile([P, PACK, Q], F32, name="q_raw")
-        nc.sync.dma_start(out=q_raw[:], in_=query.rearrange("(p t) c -> p t c", t=PACK))
-        key_words = keep.tile([P, T], U32, name="key_words", tag="keys")
-        nc.sync.dma_start(
-            out=key_words[:].bitcast(I32), in_=keys_words[0].rearrange("p n t -> p (n t)").bitcast(I32)
-        )
+        nc.sync.dma_start(out=key_bytes[0:P:8, :].bitcast(I32), in_=keys_scales[0].bitcast(I32))
+        wkey_raw = sbuf("wkey_raw", [P, PACK, M], F32)
+        nc.sync.dma_start(out=wkey_raw[:], in_=wkey.rearrange("(p t) c -> p t c", t=PACK))
         nc.sync.dma_start(out=vectors[0:1, :], in_=gb.rearrange("q o -> o q"))
         nc.sync.dma_start(out=vectors[4:8, :], in_=msz.rearrange("o (b c) -> (o b) c", c=P))
         nc.sync.dma_start(out=vectors[8:12, :], in_=size.rearrange("o (b c) -> (o b) c", c=P))
-        val_raw = {}
-        for b in range(BLOCKS):
-            val_raw[b] = keep.tile([P, T], F32, name="val_raw%d" % b, tag="val%d" % b, align_bytes=64)
-            nc.sync.dma_start(out=val_raw[b][:], in_=vals[b * P : (b + 1) * P, :])
-        wval_rows = wval.rearrange("(p t) c -> p t c", t=PACK)
-        wval_raw = []
-        for first, last in ((0, 2), (2, 3), (3, 4)):
-            piece = keep.tile([P, PACK, (last - first) * P], F32, name="wval_raw%d" % first, tag="wval_raw%d" % first, align_bytes=64)
-            nc.sync.dma_start(out=piece[:], in_=wval_rows[:, :, first * P : last * P])
-            wval_raw.extend(piece[:, :, b * P : (b + 1) * P] for b in range(last - first))
+        key_words = sbuf("key_words", [P, T], U32)
+        nc.sync.dma_start(
+            out=key_words[:].bitcast(I32), in_=keys_words[0].rearrange("p n t -> p (n t)").bitcast(I32)
+        )
 
-        zero = keep.tile([P, 1], F32, name="zero")
-        nc.vector.memset(zero[:], 0.0)
-        one = keep.tile([P, 1], F32, name="one")
-        nc.scalar.activation(one[:], zero[:], ACT.Exp)
-
-        wkey_grouped = keep.tile([P, M, PACK], BF16, name="wkey_grouped", align_bytes=64)
-        split = 192
-        interleave(nc.vector.tensor_copy, wkey_grouped[:, :split, :], wkey_raw[:, :, :split])
-        interleave(nc.scalar.copy, wkey_grouped[:, split:, :], wkey_raw[:, :, split:])
-        picked_bytes = keep.tile([P, I], U8, name="picked_bytes", tag="picked_bytes", align_bytes=64)
+        picked_bytes = sbuf("picked_bytes", [P, I], U8)
         nc.vector.tensor_copy(picked_bytes[:], key_bytes[:].indirect(offsets[:]))
-        wkey_codes, wkey_scales = mx_tiles("wkey", M, "key_bytes")
-        quantize(nc, wkey_codes[:], wkey_scales[:], wkey_grouped[:])
+        key_plane = sbuf("key_plane", [P, I], U8)
+        nc.vector.memset(key_plane[:].bitcast(I32), 0)
+        for row in range(4):
+            nc.sync.dma_start(out=key_plane[row:P:32, :].bitcast(I32), in_=picked_bytes[8 * row : P : 32, :].bitcast(I32))
 
-        q_grouped = keep.tile([P, Q, PACK], BF16, name="q_grouped", align_bytes=64)
+        def load_values(b, reuse):
+            raw = sbuf("val_raw%d" % b, [P, T], F32, reuse)
+            nc.sync.dma_start(out=raw[:], in_=vals[b * P : (b + 1) * P, :])
+            return raw
+
+        val_raw = [load_values(0, "key_bytes")]
+
+        q_grouped = sbuf("q_grouped", [P, Q, PACK], BF16)
         interleave(nc.scalar.copy, q_grouped[:], q_raw[:])
-        q_codes, q_scales = mx_tiles("q", Q)
-        quantize(nc, q_codes[:], q_scales[:], q_grouped[:])
-        picked_words = keep.tile([P, I], U32, name="picked_words", tag="picked_words", align_bytes=64)
+        q_mx = quantized("q", q_grouped[:])
+        wkey_grouped = sbuf("wkey_grouped", [P, M, PACK], BF16)
+        cut = WKEY_VECTOR_COLUMNS
+        interleave(nc.vector.tensor_copy, wkey_grouped[:, :cut, :], wkey_raw[:, :, :cut])
+        interleave(nc.scalar.copy, wkey_grouped[:, cut:, :], wkey_raw[:, :, cut:])
+        vectors_turned = psum.tile([P, P], F32, name="vectors_turned", tag="scores0")
+        nc.tensor.transpose(vectors_turned[:], vectors[:], ident[:])
+        columns = sbuf("columns", [P, 12], F32)
+        nc.vector.tensor_copy(columns[:], vectors_turned[:, 0:12])
+        gate_exp = sbuf("gate_exp", [P, 2], F32)
+        nc.scalar.activation(gate_exp[:, 0:1], columns[:, 0:1], ACT.Exp)
+        nc.scalar.activation(gate_exp[:, 1:2], columns[:, 0:1], ACT.Exp, scale=-1.0)
+        spreads = []
+        for s in range(2):
+            spread = psum.tile([P, PACK, P], F32, name="spread%d" % s, tag="spread%d" % s)
+            for t in range(PACK):
+                column = 4 * (s + 1) + t
+                nc.tensor.transpose(spread[:, t, :], columns[:, column : column + 1].to_broadcast([P, P]), ident[:])
+            spreads.append(spread)
+
+        wkey_mx = quantized("wkey", wkey_grouped[:], "vectors")
+        val_raw.append(load_values(1, "wkey_raw"))
+        val_raw.append(load_values(2, "wkey_grouped"))
+        picked_words = sbuf("picked_words", [P, I], U32)
         nc.vector.tensor_copy(picked_words[:], key_words[:].indirect(offsets[:]))
 
-        vectors_turned = psum.tile([P, P], F32, name="vectors_turned", tag="scores1")
-        nc.tensor.transpose(vectors_turned[:], vectors[:], ident[:])
-        gate = keep.tile([P, 1], F32, name="gate", tag="total0")
-        nc.scalar.copy(out=gate[:], in_=vectors_turned[:, 0:1])
-        weight_cols = keep.tile([P, 8], F32, name="weight_cols")
-        nc.scalar.copy(out=weight_cols[:], in_=vectors_turned[:, 4:12])
-        gate_exp = keep.tile([P, 2], F32, name="gate_exp")
-        nc.scalar.activation(gate_exp[:, 0:1], gate[:], ACT.Exp, scale=one[:])
-        nc.scalar.activation(gate_exp[:, 1:2], gate[:], ACT.Exp, scale=-1.0)
+        denom = sbuf("denom", [P, 2], F32)
+        probs = []
+        for s, keys_mx in enumerate((wkey_mx, (picked_words[:], key_plane[:]))):
+            scores = psum.tile([P, M], F32, name="scores%d" % s, tag="scores%d" % s)
+            product(scores[:], q_mx, keys_mx, True, True)
+            neg_max = sbuf("neg_max%d" % s, [P, 1], F32, "key_words" if s == 0 else None)
+            nc.vector.tensor_reduce(neg_max[:], scores[:], mybir.AxisListType.X, ALU.max, negate=True)
+            prob = sbuf("prob%d" % s, [P, M], F32)
+            total = sbuf("total%d" % s, [P, 1], F32)
+            nc.scalar.activation(prob[:], scores[:], ACT.Exp, bias=neg_max[:], scale=1.0, accum_out=total[:])
+            nc.scalar.activation(denom[:, s : s + 1], total[:], ACT.Identity, scale=gate_exp[:, s : s + 1], bias=total[:])
+            probs.append(prob)
+        val_raw.append(load_values(3, "key_words"))
 
-        def turn(name, rows, grouped, bank="turned", bufs=3):
+        def turn(name, rows, grouped):
             words = rows[:].bitcast(F32)
-            turned = psum.tile([P, 2, P], F32, name=name + "_turned", tag=bank, bufs=bufs)
+            turned = psum.tile([P, 2, P], F32, name=name + "_turned", tag="turned", bufs=4)
             for u in range(2):
                 nc.tensor.transpose(turned[:, u, :], words[:, u : 2 * P : 2], ident[:])
             nc.scalar.copy(
@@ -118,32 +141,8 @@ def tile_attend_knn_memory_kernel(tc, query, wkey, wval, keys_words, keys_scales
                 in_=turned[:].rearrange("p u c -> p c u"),
             )
 
-        denom = keep.tile([P, 2], F32, name="denom")
-        probs = []
-        for s, (key_codes, key_scales) in enumerate(((wkey_codes, wkey_scales), (picked_words, picked_bytes))):
-            scores = psum.tile([P, M], F32, name="scores%d" % s, tag="scores%d" % s)
-            nc.tensor.matmul_mx(
-                out=scores[:], lhsT=q_codes[:].bitcast(FP8X4), lhsT_scale=q_scales[:],
-                rhs=key_codes[:].bitcast(FP8X4), rhs_scale=key_scales[:], start=True, stop=True,
-            )
-            neg_max = keep.tile([P, 1], F32, name="neg_max%d" % s, tag=("keys", "neg_max1")[s])
-            nc.vector.tensor_reduce(neg_max[:], scores[:], mybir.AxisListType.X, ALU.max, negate=True)
-            prob = keep.tile([P, M], F32, name="prob%d" % s, tag="prob%d" % s, align_bytes=64)
-            total = keep.tile([P, 1], F32, name="total%d" % s, tag="total%d" % s)
-            nc.scalar.activation(prob[:], scores[:], ACT.Exp, bias=neg_max[:], scale=1.0, accum_out=total[:])
-            nc.scalar.activation(denom[:, s : s + 1], total[:], ACT.Identity, scale=gate_exp[:, s : s + 1], bias=total[:])
-            probs.append(prob)
-
-        columns = weight_cols
-        spreads = []
-        for s in range(2):
-            spread = psum.tile([P, PACK, P], F32, name="spread%d" % s, tag="sums%d" % (2 + s))
-            for t in range(PACK):
-                nc.tensor.transpose(spread[:, t, :], columns[:, 4 * s + t : 4 * s + t + 1].to_broadcast([P, P]), ident[:])
-            spreads.append(spread)
-
         def pick_values(b, vector_slots):
-            picked = keep.tile([P, I], BF16, name="picked%d" % b, align_bytes=64)
+            picked = sbuf("picked%d" % b, [P, I], BF16)
             cut = vector_slots // 16
             if vector_slots > 0:
                 nc.vector.tensor_copy(picked[:, :vector_slots], val_raw[b][:].indirect(offsets[:, :cut]))
@@ -151,70 +150,60 @@ def tile_attend_knn_memory_kernel(tc, query, wkey, wval, keys_words, keys_scales
                 nc.scalar.activation(picked[:, vector_slots:], val_raw[b][:].indirect(offsets[:, cut:]), ACT.Copy)
             return picked
 
-        def grouped_tile(name, width, tag=None):
-            return keep.tile([P, width, PACK], BF16, name=name, tag=tag or name, align_bytes=64)
-
-        def quantized(name, grouped, tag=None):
-            codes, scales = mx_tiles(name, grouped.shape[1], tag)
-            quantize(nc, codes[:], scales[:], grouped)
-            return codes, scales
-
-        val_mx = {}
         picked0 = pick_values(0, I)
         picked1 = pick_values(1, 0)
-        mid_grouped = grouped_tile("mid_grouped", 4 * P, "val1")
+        mid_grouped = sbuf("mid_grouped", [P, 4 * P, PACK], BF16, "wkey_raw")
         turn("val0", picked0, mid_grouped[:, 2 * P : 3 * P, :])
-        factor = keep.tile([P, 2], F32, name="factor")
+        factor = sbuf("factor", [P, 2], F32)
         nc.vector.reciprocal(factor[:], denom[:])
         for s in range(2):
-            rows = keep.tile([P, M], BF16, name="rows%d" % s, align_bytes=64)
+            rows = sbuf("rows%d" % s, [P, M], BF16)
             nc.vector.scalar_tensor_tensor(
-                out=rows[:],
-                in0=probs[s][:],
-                scalar=factor[:, s : s + 1],
-                in1=spreads[s][:].rearrange("p b c -> p (b c)"),
-                op0=ALU.mult, op1=ALU.mult,
+                out=rows[:], in0=probs[s][:], scalar=factor[:, s : s + 1],
+                in1=spreads[s][:].rearrange("p b c -> p (b c)"), op0=ALU.mult, op1=ALU.mult,
             )
             turn("rows%d" % s, rows, mid_grouped[:, s * Q : (s + 1) * Q, :])
         turn("val1", picked1, mid_grouped[:, 3 * P :, :])
-        pair_grouped = grouped_tile("pair_grouped", 2 * P)
-        turn("val2", pick_values(2, I), pair_grouped[:, :P, :])
-        mid_codes, mid_scales = quantized("mid", mid_grouped[:], "val2")
-        for b in range(2):
-            cols = slice((b + 2) * P, (b + 3) * P)
-            val_mx[b] = (mid_codes[:, cols], mid_scales[:, cols])
-        picked3 = pick_values(3, SHARE)
 
-        wval_mx = {}
-        interleave(nc.vector.tensor_copy, pair_grouped[:, P:, :], wval_raw[0][:])
-        pair_codes, pair_scales = quantized("pair", pair_grouped[:])
-        val_mx[2] = (pair_codes[:, :P], pair_scales[:, :P])
-        wval_mx[0] = (pair_codes[:, P:], pair_scales[:, P:])
-        wval_grouped = {b: grouped_tile("wval_grouped%d" % b, P) for b in (1, 2, 3)}
-        interleave(nc.scalar.copy, wval_grouped[1][:], wval_raw[1][:])
-        grouped3 = grouped_tile("val_grouped3", P, "wval_raw0")
-        turn("val3", picked3, grouped3[:], "last_turned", 1)
-        interleave(nc.vector.tensor_copy, wval_grouped[2][:], wval_raw[2][:])
-        interleave(nc.scalar.copy, wval_grouped[3][:], wval_raw[3][:])
-        for b in (1, 2):
-            wval_mx[b] = quantized("wval%d" % b, wval_grouped[b][:])
-        val_mx[3] = quantized("val3", grouped3[:])
-        wval_mx[3] = quantized("wval3", wval_grouped[3][:])
+        wval_rows = wval.rearrange("(p t) c -> p t c", t=PACK)
+        wval_raw = []
+        for first, last, reuse in ((0, 3, "key_bytes"), (3, 4, "prob1")):
+            piece = sbuf("wval_raw%d" % first, [P, PACK, (last - first) * P], F32, reuse)
+            nc.sync.dma_start(out=piece[:], in_=wval_rows[:, :, first * P : last * P])
+            wval_raw.extend(piece[:, :, b * P : (b + 1) * P] for b in range(last - first))
 
-        window_weights = (mid_codes[:, :Q], mid_scales[:, :Q])
-        memory_weights = (mid_codes[:, Q : 2 * Q], mid_scales[:, Q : 2 * Q])
-        banks = ("last_turned", "scores1", "sums2", "sums3")
-        result = keep.tile([P, E], F32, name="result")
-        for b in range(BLOCKS):
+        grouped2 = sbuf("val_grouped2", [P, P, PACK], BF16)
+        turn("val2", pick_values(2, I), grouped2[:])
+        mid_mx = quantized("mid", mid_grouped[:], "wkey_grouped")
+        window_weights, memory_weights = columns_of(mid_mx, 0), columns_of(mid_mx, Q)
+        val_mx = [columns_of(mid_mx, 2 * P), columns_of(mid_mx, 3 * P)]
+        pair_grouped = sbuf("pair_grouped", [P, 2 * P, PACK], BF16)
+        turn("val3", pick_values(3, LAST_GATHER_VECTOR_SLOTS), pair_grouped[:, :P, :])
+        val_mx.append(quantized("val2", grouped2[:], "key_words"))
+
+        first_grouped = sbuf("wval_grouped0", [P, P, PACK], BF16)
+        interleave(nc.vector.tensor_copy, first_grouped[:], wval_raw[0])
+        interleave(nc.vector.tensor_copy, pair_grouped[:, P:, :], wval_raw[1])
+        wval_mx = [quantized("wval0", first_grouped[:])]
+        pair_mx = quantized("pair", pair_grouped[:])
+        val_mx.append(columns_of(pair_mx, 0))
+        wval_mx.append(columns_of(pair_mx, P))
+        third_grouped = sbuf("wval_grouped2", [P, P, PACK], BF16)
+        cut = WVAL2_SCALAR_COLUMNS
+        interleave(nc.scalar.copy, third_grouped[:, :cut, :], wval_raw[2][:, :, :cut])
+        interleave(nc.vector.tensor_copy, third_grouped[:, cut:, :], wval_raw[2][:, :, cut:])
+        wval_mx.append(quantized("wval2", third_grouped[:]))
+        last_grouped = sbuf("wval_grouped3", [P, P, PACK], BF16)
+        interleave(nc.scalar.copy, last_grouped[:], wval_raw[3])
+        wval_mx.append(quantized("wval3", last_grouped[:]))
+
+        result = sbuf("result", [P, E], F32, "prob1")
+        for b, bank in enumerate(("scores0", "scores1", "spread0", "spread1")):
             cols = slice(b * P, (b + 1) * P)
-            acc = psum.tile([P, P], F32, name="acc%d" % b, tag=banks[b])
-            passes = [(memory_weights, val_mx[b]), (window_weights, wval_mx[b])]
-            for n, ((w_codes, w_scales), (v_codes, v_scales)) in enumerate(passes):
-                nc.tensor.matmul_mx(
-                    out=acc[:], lhsT=w_codes.bitcast(FP8X4), lhsT_scale=w_scales,
-                    rhs=v_codes[:].bitcast(FP8X4), rhs_scale=v_scales[:], start=n == 0, stop=n == 1,
-                )
-            (nc.vector.tensor_copy if b == 3 else nc.scalar.copy)(out=result[:, cols], in_=acc[:])
+            acc = psum.tile([P, P], F32, name="acc%d" % b, tag=bank)
+            product(acc[:], memory_weights, val_mx[b], True, False)
+            product(acc[:], window_weights, wval_mx[b], False, True)
+            (nc.vector.tensor_copy if b == BLOCKS - 1 else nc.scalar.copy)(out=result[:, cols], in_=acc[:])
             if b > 0:
                 stored = slice(0 if b == 1 else b * P, (b + 1) * P)
                 nc.sync.dma_start(out=out[:, stored], in_=result[:, stored])

@@ -32,9 +32,12 @@ def tile_attend_knn_memory_kernel(tc, query, wkey, wval, keys_words, keys_scales
     nc = tc.nc
     with ExitStack() as ctx:
         keep = ctx.enter_context(tc.tile_pool(name="keep", bufs=1))
+        shared = ctx.enter_context(tc.tile_pool(name="shared", bufs=1))
         psum = ctx.enter_context(tc.psum_pool(name="psum", bufs=1))
 
         def sbuf(name, shape, dtype, reuse=None):
+            if isinstance(reuse, int):
+                return shared.tile(shape, dtype, name=name, offset=reuse, align_bytes=64)
             return keep.tile(shape, dtype, name=name, tag=reuse or name, align_bytes=64)
 
         def quantized(name, grouped, reuse=None):
@@ -53,7 +56,7 @@ def tile_attend_knn_memory_kernel(tc, query, wkey, wval, keys_words, keys_scales
                 rhs=moving[0].bitcast(FP8X4), rhs_scale=moving[1], start=start, stop=stop,
             )
 
-        key_bytes = sbuf("key_bytes", [P, T], U8)
+        key_bytes = sbuf("key_bytes", [P, T], U8, 0)
         nc.gpsimd.memset(key_bytes[:].bitcast(I32), 0)
         vectors = sbuf("vectors", [P, P], F32)
         nc.vector.memset(vectors[:], 0.0)
@@ -87,7 +90,9 @@ def tile_attend_knn_memory_kernel(tc, query, wkey, wval, keys_words, keys_scales
             nc.sync.dma_start(out=raw[:], in_=vals[b * P : (b + 1) * P, :])
             return raw
 
-        val_raw = [load_values(0, "key_bytes")]
+        pair_raw = sbuf("val_raw01", [P, 2 * T], F32, 0)
+        nc.sync.dma_start(out=pair_raw[:], in_=vals[0 : 2 * P, :].rearrange("(p j) t -> p (j t)", j=2))
+        val_raw = {}
 
         q_grouped = sbuf("q_grouped", [P, Q, PACK], BF16)
         interleave(nc.scalar.copy, q_grouped[:], q_raw[:])
@@ -112,8 +117,7 @@ def tile_attend_knn_memory_kernel(tc, query, wkey, wval, keys_words, keys_scales
             spreads.append(spread)
 
         wkey_mx = quantized("wkey", wkey_grouped[:], "vectors")
-        val_raw.append(load_values(1, "wkey_raw"))
-        val_raw.append(load_values(2, "wkey_grouped"))
+        val_raw[2] = load_values(2, "wkey_grouped")
         picked_words = sbuf("picked_words", [P, I], U32)
         nc.vector.tensor_copy(picked_words[:], key_words[:].indirect(offsets[:]))
 
@@ -129,7 +133,7 @@ def tile_attend_knn_memory_kernel(tc, query, wkey, wval, keys_words, keys_scales
             nc.scalar.activation(prob[:], scores[:], ACT.Exp, bias=neg_max[:], scale=1.0, accum_out=total[:])
             nc.scalar.activation(denom[:, s : s + 1], total[:], ACT.Identity, scale=gate_exp[:, s : s + 1], bias=total[:])
             probs.append(prob)
-        val_raw.append(load_values(3, "key_words"))
+        val_raw[3] = load_values(3, "key_words")
 
         def turn(name, rows, grouped):
             words = rows[:].bitcast(F32)
@@ -142,7 +146,7 @@ def tile_attend_knn_memory_kernel(tc, query, wkey, wval, keys_words, keys_scales
             )
 
         def pick_values(b, vector_slots):
-            picked = sbuf("picked%d" % b, [P, I], BF16)
+            picked = sbuf("picked%d" % b, [P, I], BF16, "picked_odd" if b == 3 else 4096)
             cut = vector_slots // 16
             if vector_slots > 0:
                 nc.vector.tensor_copy(picked[:, :vector_slots], val_raw[b][:].indirect(offsets[:, :cut]))
@@ -150,36 +154,51 @@ def tile_attend_knn_memory_kernel(tc, query, wkey, wval, keys_words, keys_scales
                 nc.scalar.activation(picked[:, vector_slots:], val_raw[b][:].indirect(offsets[:, cut:]), ACT.Copy)
             return picked
 
-        picked0 = pick_values(0, I)
-        picked1 = pick_values(1, 0)
-        mid_grouped = sbuf("mid_grouped", [P, 4 * P, PACK], BF16, "wkey_raw")
-        turn("val0", picked0, mid_grouped[:, 2 * P : 3 * P, :])
+        mid_grouped = sbuf("mid_grouped", [P, 2 * P, PACK], BF16, 0)
+        val_grouped = sbuf("val_grouped", [P, 3 * P, PACK], BF16)
+        weight_rows = []
         factor = sbuf("factor", [P, 2], F32)
-        nc.vector.reciprocal(factor[:], denom[:])
         for s in range(2):
+            nc.vector.reciprocal(factor[:, s : s + 1], denom[:, s : s + 1])
             rows = sbuf("rows%d" % s, [P, M], BF16)
             nc.vector.scalar_tensor_tensor(
                 out=rows[:], in0=probs[s][:], scalar=factor[:, s : s + 1],
                 in1=spreads[s][:].rearrange("p b c -> p (b c)"), op0=ALU.mult, op1=ALU.mult,
             )
-            turn("rows%d" % s, rows, mid_grouped[:, s * Q : (s + 1) * Q, :])
-        turn("val1", picked1, mid_grouped[:, 3 * P :, :])
+            weight_rows.append(rows)
+
+        even = sbuf("picked_even", [P, I], BF16, "total1")
+        nc.scalar.activation(even[:], pair_raw[:].indirect(offsets[:]), ACT.Copy)
+        odd = sbuf("picked_odd", [P, 2, P, 2], BF16)
+        nc.vector.tensor_copy(odd[:].rearrange("p u s e -> p s u e"), pair_raw[:, T:].indirect(offsets[:]))
+        for s in range(2):
+            turn("rows%d" % s, weight_rows[s], mid_grouped[:, s * Q : (s + 1) * Q, :])
+        pair_turned = psum.tile([P, 2, 2, P], F32, name="pair_turned", tag="turned", bufs=4)
+        odd_words = odd[:].rearrange("p u s e -> p (u s e)").bitcast(F32)
+        even_words = even[:].bitcast(F32)
+        for u in range(2):
+            nc.tensor.transpose(pair_turned[:, 1, u, :], odd_words[:, u * P : (u + 1) * P], ident[:])
+        for u in range(2):
+            nc.tensor.transpose(pair_turned[:, 0, u, :], even_words[:, u : 2 * P : 2], ident[:])
+        nc.scalar.copy(
+            out=val_grouped[:, : 2 * P, :].rearrange("p c t -> p (c t)").bitcast(F32).rearrange("p (c j u) -> p c j u", j=2, u=2),
+            in_=pair_turned[:].rearrange("p j u c -> p c j u"),
+        )
 
         wval_rows = wval.rearrange("(p t) c -> p t c", t=PACK)
         wval_raw = []
-        for first, last, reuse in ((0, 3, "key_bytes"), (3, 4, "prob1")):
+        for first, last, reuse in ((0, 3, "prob0"), (3, 4, "prob1")):
             piece = sbuf("wval_raw%d" % first, [P, PACK, (last - first) * P], F32, reuse)
             nc.sync.dma_start(out=piece[:], in_=wval_rows[:, :, first * P : last * P])
             wval_raw.extend(piece[:, :, b * P : (b + 1) * P] for b in range(last - first))
 
-        grouped2 = sbuf("val_grouped2", [P, P, PACK], BF16)
-        turn("val2", pick_values(2, I), grouped2[:])
+        turn("val2", pick_values(2, I), val_grouped[:, 2 * P :, :])
         mid_mx = quantized("mid", mid_grouped[:], "wkey_grouped")
         window_weights, memory_weights = columns_of(mid_mx, 0), columns_of(mid_mx, Q)
-        val_mx = [columns_of(mid_mx, 2 * P), columns_of(mid_mx, 3 * P)]
         pair_grouped = sbuf("pair_grouped", [P, 2 * P, PACK], BF16)
         turn("val3", pick_values(3, LAST_GATHER_VECTOR_SLOTS), pair_grouped[:, :P, :])
-        val_mx.append(quantized("val2", grouped2[:], "key_words"))
+        early_mx = quantized("val012", val_grouped[:], "key_words")
+        val_mx = [columns_of(early_mx, b * P) for b in range(3)]
 
         first_grouped = sbuf("wval_grouped0", [P, P, PACK], BF16)
         interleave(nc.vector.tensor_copy, first_grouped[:], wval_raw[0])

@@ -81,8 +81,8 @@ def tile_attend_knn_memory_kernel(tc, query, wkey, wval, keys_words, keys_scales
         picked_bytes = sbuf("picked_bytes", [P, I], U8)
         nc.vector.tensor_copy(picked_bytes[:], key_bytes[:].indirect(offsets[:]))
         key_plane = sbuf("key_plane", [P, I], U8)
-        nc.vector.memset(key_plane[:].bitcast(I32), 0)
-        for row in range(4):
+        nc.vector.tensor_copy(key_plane[:].bitcast(I32), picked_bytes[:].bitcast(I32))
+        for row in range(1, 4):
             nc.sync.dma_start(out=key_plane[row:P:32, :].bitcast(I32), in_=picked_bytes[8 * row : P : 32, :].bitcast(I32))
 
         def load_values(b, reuse):

@@ -146,7 +146,7 @@ def tile_attend_knn_memory_kernel(tc, query, wkey, wval, keys_words, keys_scales
             )
 
         def pick_values(b, vector_slots):
-            picked = sbuf("picked%d" % b, [P, I], BF16, "picked_odd" if b == 3 else 4096)
+            picked = sbuf("picked%d" % b, [P, I], BF16, "picked_odd" if b == 3 else "denom")
             cut = vector_slots // 16
             if vector_slots > 0:
                 nc.vector.tensor_copy(picked[:, :vector_slots], val_raw[b][:].indirect(offsets[:, :cut]))

@@ -37,8 +37,8 @@ def tile_attend_knn_memory_kernel(tc, query, wkey, wval, keys_words, keys_scales
 
         def sbuf(name, shape, dtype, reuse=None):
             if isinstance(reuse, int):
-                return shared.tile(shape, dtype, name=name, offset=reuse, align_bytes=64)
-            return keep.tile(shape, dtype, name=name, tag=reuse or name, align_bytes=64)
+                return shared.tile(shape, dtype, name=name, offset=reuse, align_bytes=256)
+            return keep.tile(shape, dtype, name=name, tag=reuse or name, align_bytes=256)
 
         def quantized(name, grouped, reuse=None):
             width = grouped.shape[1]

@@ -21,7 +21,7 @@ PACK = 4
 BLOCKS = E // P
 WKEY_VECTOR_COLUMNS = 288
 LAST_GATHER_VECTOR_SLOTS = 320
-WVAL2_SCALAR_COLUMNS = 64
+LAST_PIECE_VECTOR_COLUMNS = 32
 
 
 def interleave(copy, dst, src):
@@ -187,7 +187,7 @@ def tile_attend_knn_memory_kernel(tc, query, wkey, wval, keys_words, keys_scales
 
         wval_rows = wval.rearrange("(p t) c -> p t c", t=PACK)
         wval_raw = []
-        for first, last, reuse in ((0, 3, "prob0"), (3, 4, "prob1")):
+        for first, last, reuse in ((0, 1, "prob0"), (1, 3, "rows0"), (3, 4, "prob1")):
             piece = sbuf("wval_raw%d" % first, [P, PACK, (last - first) * P], F32, reuse)
             nc.sync.dma_start(out=piece[:], in_=wval_rows[:, :, first * P : last * P])
             wval_raw.extend(piece[:, :, b * P : (b + 1) * P] for b in range(last - first))
@@ -195,25 +195,26 @@ def tile_attend_knn_memory_kernel(tc, query, wkey, wval, keys_words, keys_scales
         turn("val2", pick_values(2, I), val_grouped[:, 2 * P :, :])
         mid_mx = quantized("mid", mid_grouped[:], "wkey_grouped")
         window_weights, memory_weights = columns_of(mid_mx, 0), columns_of(mid_mx, Q)
-        pair_grouped = sbuf("pair_grouped", [P, 2 * P, PACK], BF16)
-        turn("val3", pick_values(3, LAST_GATHER_VECTOR_SLOTS), pair_grouped[:, :P, :])
+        picked3 = pick_values(3, LAST_GATHER_VECTOR_SLOTS)
+        first_grouped = sbuf("wval_grouped0", [P, P, PACK], BF16)
+        interleave(nc.scalar.copy, first_grouped[:], wval_raw[0])
+        grouped3 = sbuf("val_grouped3", [P, P, PACK], BF16, "prob0")
+        turn("val3", picked3, grouped3[:])
         early_mx = quantized("val012", val_grouped[:], "key_words")
         val_mx = [columns_of(early_mx, b * P) for b in range(3)]
 
-        first_grouped = sbuf("wval_grouped0", [P, P, PACK], BF16)
-        interleave(nc.vector.tensor_copy, first_grouped[:], wval_raw[0])
-        interleave(nc.vector.tensor_copy, pair_grouped[:, P:, :], wval_raw[1])
-        wval_mx = [quantized("wval0", first_grouped[:])]
-        pair_mx = quantized("pair", pair_grouped[:])
-        val_mx.append(columns_of(pair_mx, 0))
-        wval_mx.append(columns_of(pair_mx, P))
+        second_grouped = sbuf("wval_grouped1", [P, P, PACK], BF16)
         third_grouped = sbuf("wval_grouped2", [P, P, PACK], BF16)
-        cut = WVAL2_SCALAR_COLUMNS
-        interleave(nc.scalar.copy, third_grouped[:, :cut, :], wval_raw[2][:, :, :cut])
-        interleave(nc.vector.tensor_copy, third_grouped[:, cut:, :], wval_raw[2][:, :, cut:])
-        wval_mx.append(quantized("wval2", third_grouped[:]))
         last_grouped = sbuf("wval_grouped3", [P, P, PACK], BF16)
-        interleave(nc.scalar.copy, last_grouped[:], wval_raw[3])
+        wval_mx = [quantized("wval0", first_grouped[:])]
+        interleave(nc.vector.tensor_copy, second_grouped[:], wval_raw[1])
+        interleave(nc.vector.tensor_copy, third_grouped[:], wval_raw[2])
+        wval_mx.append(quantized("wval1", second_grouped[:]))
+        cut = LAST_PIECE_VECTOR_COLUMNS
+        interleave(nc.vector.tensor_copy, last_grouped[:, :cut, :], wval_raw[3][:, :, :cut])
+        interleave(nc.scalar.copy, last_grouped[:, cut:, :], wval_raw[3][:, :, cut:])
+        val_mx.append(quantized("val3", grouped3[:]))
+        wval_mx.append(quantized("wval2", third_grouped[:]))
         wval_mx.append(quantized("wval3", last_grouped[:]))
 
         result = sbuf("result", [P, E], F32, "prob1")

@@ -18,6 +18,7 @@ ACT = mybir.ActivationFunctionType
 
 P = 128
 PACK = 4
+WINDOW = T * 4
 BLOCKS = E // P
 WKEY_VECTOR_COLUMNS = 288
 LAST_GATHER_VECTOR_SLOTS = 320
@@ -68,7 +69,7 @@ def tile_attend_knn_memory_kernel(tc, query, wkey, wval, keys_words, keys_scales
         offsets = keep.tile([P, I // 16], U16, name="offsets")
         nc.sync.dma_start(offsets[:], offs)
         nc.sync.dma_start(out=key_bytes[0:P:8, :].bitcast(I32), in_=keys_scales[0].bitcast(I32))
-        wkey_raw = sbuf("wkey_raw", [P, PACK, M], F32)
+        wkey_raw = sbuf("wkey_raw", [P, PACK, M], F32, WINDOW)
         nc.sync.dma_start(out=wkey_raw[:], in_=wkey.rearrange("(p t) c -> p t c", t=PACK))
         nc.sync.dma_start(out=vectors[0:1, :], in_=gb.rearrange("q o -> o q"))
         nc.sync.dma_start(out=vectors[4:8, :], in_=msz.rearrange("o (b c) -> (o b) c", c=P))
@@ -90,17 +91,16 @@ def tile_attend_knn_memory_kernel(tc, query, wkey, wval, keys_words, keys_scales
             nc.sync.dma_start(out=raw[:], in_=vals[b * P : (b + 1) * P, :])
             return raw
 
-        pair_raw = sbuf("val_raw01", [P, 2 * T], F32, 0)
-        nc.sync.dma_start(out=pair_raw[:], in_=vals[0 : 2 * P, :].rearrange("(p j) t -> p (j t)", j=2))
-        val_raw = {}
+        val_raw = {0: load_values(0, 0)}
 
         q_grouped = sbuf("q_grouped", [P, Q, PACK], BF16)
         interleave(nc.scalar.copy, q_grouped[:], q_raw[:])
         q_mx = quantized("q", q_grouped[:])
-        wkey_grouped = sbuf("wkey_grouped", [P, M, PACK], BF16)
+        wkey_grouped = sbuf("wkey_grouped", [P, M, PACK], BF16, 2 * WINDOW)
         cut = WKEY_VECTOR_COLUMNS
         interleave(nc.vector.tensor_copy, wkey_grouped[:, :cut, :], wkey_raw[:, :, :cut])
         interleave(nc.scalar.copy, wkey_grouped[:, cut:, :], wkey_raw[:, :, cut:])
+        val_raw[1] = load_values(1, WINDOW)
         vectors_turned = psum.tile([P, P], F32, name="vectors_turned", tag="scores0")
         nc.tensor.transpose(vectors_turned[:], vectors[:], ident[:])
         columns = sbuf("columns", [P, 12], F32)
@@ -117,7 +117,7 @@ def tile_attend_knn_memory_kernel(tc, query, wkey, wval, keys_words, keys_scales
             spreads.append(spread)
 
         wkey_mx = quantized("wkey", wkey_grouped[:], "vectors")
-        val_raw[2] = load_values(2, "wkey_grouped")
+        val_raw[2] = load_values(2, 2 * WINDOW)
         picked_words = sbuf("picked_words", [P, I], U32)
         nc.vector.tensor_copy(picked_words[:], key_words[:].indirect(offsets[:]))
 
@@ -145,8 +145,8 @@ def tile_attend_knn_memory_kernel(tc, query, wkey, wval, keys_words, keys_scales
                 in_=turned[:].rearrange("p u c -> p c u"),
             )
 
-        def pick_values(b, vector_slots):
-            picked = sbuf("picked%d" % b, [P, I], BF16, "picked_odd" if b == 3 else "denom")
+        def pick_values(b, vector_slots, reuse):
+            picked = sbuf("picked%d" % b, [P, I], BF16, reuse)
             cut = vector_slots // 16
             if vector_slots > 0:
                 nc.vector.tensor_copy(picked[:, :vector_slots], val_raw[b][:].indirect(offsets[:, :cut]))
@@ -154,54 +154,43 @@ def tile_attend_knn_memory_kernel(tc, query, wkey, wval, keys_words, keys_scales
                 nc.scalar.activation(picked[:, vector_slots:], val_raw[b][:].indirect(offsets[:, cut:]), ACT.Copy)
             return picked
 
-        mid_grouped = sbuf("mid_grouped", [P, 2 * P, PACK], BF16, 0)
-        val_grouped = sbuf("val_grouped", [P, 3 * P, PACK], BF16)
+        picked0 = pick_values(0, I, "picked_words")
+        early_grouped = sbuf("early_grouped", [P, 4 * P, PACK], BF16, WINDOW)
+        grouped2 = sbuf("val_grouped2", [P, P, PACK], BF16)
         weight_rows = []
         factor = sbuf("factor", [P, 2], F32)
         for s in range(2):
             nc.vector.reciprocal(factor[:, s : s + 1], denom[:, s : s + 1])
-            rows = sbuf("rows%d" % s, [P, M], BF16)
+            rows = sbuf("rows%d" % s, [P, M], BF16, 0 if s == 0 else None)
             nc.vector.scalar_tensor_tensor(
                 out=rows[:], in0=probs[s][:], scalar=factor[:, s : s + 1],
                 in1=spreads[s][:].rearrange("p b c -> p (b c)"), op0=ALU.mult, op1=ALU.mult,
             )
             weight_rows.append(rows)
 
-        even = sbuf("picked_even", [P, I], BF16, "total1")
-        nc.scalar.activation(even[:], pair_raw[:].indirect(offsets[:]), ACT.Copy)
-        odd = sbuf("picked_odd", [P, 2, P, 2], BF16)
-        nc.vector.tensor_copy(odd[:].rearrange("p u s e -> p s u e"), pair_raw[:, T:].indirect(offsets[:]))
+        picked1 = pick_values(1, 0, "total1")
+        turn("val0", picked0, early_grouped[:, 2 * P : 3 * P, :])
         for s in range(2):
-            turn("rows%d" % s, weight_rows[s], mid_grouped[:, s * Q : (s + 1) * Q, :])
-        pair_turned = psum.tile([P, 2, 2, P], F32, name="pair_turned", tag="turned", bufs=4)
-        odd_words = odd[:].rearrange("p u s e -> p (u s e)").bitcast(F32)
-        even_words = even[:].bitcast(F32)
-        for u in range(2):
-            nc.tensor.transpose(pair_turned[:, 1, u, :], odd_words[:, u * P : (u + 1) * P], ident[:])
-        for u in range(2):
-            nc.tensor.transpose(pair_turned[:, 0, u, :], even_words[:, u : 2 * P : 2], ident[:])
-        nc.scalar.copy(
-            out=val_grouped[:, : 2 * P, :].rearrange("p c t -> p (c t)").bitcast(F32).rearrange("p (c j u) -> p c j u", j=2, u=2),
-            in_=pair_turned[:].rearrange("p j u c -> p c j u"),
-        )
+            turn("rows%d" % s, weight_rows[s], early_grouped[:, s * Q : (s + 1) * Q, :])
+        turn("val1", picked1, early_grouped[:, 3 * P :, :])
 
         wval_rows = wval.rearrange("(p t) c -> p t c", t=PACK)
         wval_raw = []
-        for first, last, reuse in ((0, 1, "prob0"), (1, 3, "rows0"), (3, 4, "prob1")):
+        for first, last, reuse in ((0, 1, "prob0"), (1, 3, "rows1"), (3, 4, "prob1")):
             piece = sbuf("wval_raw%d" % first, [P, PACK, (last - first) * P], F32, reuse)
             nc.sync.dma_start(out=piece[:], in_=wval_rows[:, :, first * P : last * P])
             wval_raw.extend(piece[:, :, b * P : (b + 1) * P] for b in range(last - first))
 
-        turn("val2", pick_values(2, I), val_grouped[:, 2 * P :, :])
-        mid_mx = quantized("mid", mid_grouped[:], "wkey_grouped")
+        turn("val2", pick_values(2, I, "denom"), grouped2[:])
+        mid_mx = quantized("early", early_grouped[:], 2 * WINDOW)
         window_weights, memory_weights = columns_of(mid_mx, 0), columns_of(mid_mx, Q)
-        picked3 = pick_values(3, LAST_GATHER_VECTOR_SLOTS)
+        picked3 = pick_values(3, LAST_GATHER_VECTOR_SLOTS, "picked_words")
         first_grouped = sbuf("wval_grouped0", [P, P, PACK], BF16)
         interleave(nc.scalar.copy, first_grouped[:], wval_raw[0])
         grouped3 = sbuf("val_grouped3", [P, P, PACK], BF16, "prob0")
         turn("val3", picked3, grouped3[:])
-        early_mx = quantized("val012", val_grouped[:], "key_words")
-        val_mx = [columns_of(early_mx, b * P) for b in range(3)]
+        val_mx = [columns_of(mid_mx, (2 + b) * P) for b in range(2)]
+        val_mx.append(quantized("val2", grouped2[:], "key_words"))
 
         second_grouped = sbuf("wval_grouped1", [P, P, PACK], BF16)
         third_grouped = sbuf("wval_grouped2", [P, P, PACK], BF16)

@@ -135,12 +135,12 @@ def tile_attend_knn_memory_kernel(tc, query, wkey, wval, keys_words, keys_scales
             probs.append(prob)
         val_raw[3] = load_values(3, "key_words")
 
-        def turn(name, rows, grouped):
+        def turn(name, rows, grouped, copy=nc.scalar.copy):
             words = rows[:].bitcast(F32)
             turned = psum.tile([P, 2, P], F32, name=name + "_turned", tag="turned", bufs=4)
             for u in range(2):
                 nc.tensor.transpose(turned[:, u, :], words[:, u : 2 * P : 2], ident[:])
-            nc.scalar.copy(
+            copy(
                 out=grouped.rearrange("p c t -> p (c t)").bitcast(F32).rearrange("p (c u) -> p c u", u=2),
                 in_=turned[:].rearrange("p u c -> p c u"),
             )
@@ -158,10 +158,10 @@ def tile_attend_knn_memory_kernel(tc, query, wkey, wval, keys_words, keys_scales
         early_grouped = sbuf("early_grouped", [P, 4 * P, PACK], BF16, WINDOW)
         grouped2 = sbuf("val_grouped2", [P, P, PACK], BF16)
         weight_rows = []
-        factor = sbuf("factor", [P, 2], F32)
+        factor = sbuf("factor", [P, 2], F32, 0)
         for s in range(2):
             nc.vector.reciprocal(factor[:, s : s + 1], denom[:, s : s + 1])
-            rows = sbuf("rows%d" % s, [P, M], BF16, 0 if s == 0 else None)
+            rows = sbuf("rows%d" % s, [P, M], BF16)
             nc.vector.scalar_tensor_tensor(
                 out=rows[:], in0=probs[s][:], scalar=factor[:, s : s + 1],
                 in1=spreads[s][:].rearrange("p b c -> p (b c)"), op0=ALU.mult, op1=ALU.mult,
@@ -169,7 +169,7 @@ def tile_attend_knn_memory_kernel(tc, query, wkey, wval, keys_words, keys_scales
             weight_rows.append(rows)
 
         picked1 = pick_values(1, 0, "total1")
-        turn("val0", picked0, early_grouped[:, 2 * P : 3 * P, :])
+        turn("val0", picked0, early_grouped[:, 2 * P : 3 * P, :], nc.vector.tensor_copy)
         for s in range(2):
             turn("rows%d" % s, weight_rows[s], early_grouped[:, s * Q : (s + 1) * Q, :])
         turn("val1", picked1, early_grouped[:, 3 * P :, :])

@@ -22,7 +22,7 @@ WINDOW = T * 4
 BLOCKS = E // P
 WKEY_VECTOR_COLUMNS = 288
 LAST_GATHER_VECTOR_SLOTS = 320
-LAST_PIECE_VECTOR_COLUMNS = 32
+LAST_PIECE_VECTOR_COLUMNS = 48
 
 
 def interleave(copy, dst, src):
@@ -155,8 +155,8 @@ def tile_attend_knn_memory_kernel(tc, query, wkey, wval, keys_words, keys_scales
             return picked
 
         picked0 = pick_values(0, I, "picked_words")
-        early_grouped = sbuf("early_grouped", [P, 4 * P, PACK], BF16, WINDOW)
-        grouped2 = sbuf("val_grouped2", [P, P, PACK], BF16)
+        early_grouped = sbuf("early_grouped", [P, 3 * P, PACK], BF16, WINDOW)
+        middle_grouped = sbuf("middle_grouped", [P, 2 * P, PACK], BF16)
         weight_rows = []
         factor = sbuf("factor", [P, 2], F32, 0)
         for s in range(2):
@@ -169,19 +169,19 @@ def tile_attend_knn_memory_kernel(tc, query, wkey, wval, keys_words, keys_scales
             weight_rows.append(rows)
 
         picked1 = pick_values(1, 0, "total1")
-        turn("val0", picked0, early_grouped[:, 2 * P : 3 * P, :], nc.vector.tensor_copy)
+        turn("val0", picked0, early_grouped[:, 2 * P :, :], nc.vector.tensor_copy)
         for s in range(2):
             turn("rows%d" % s, weight_rows[s], early_grouped[:, s * Q : (s + 1) * Q, :])
-        turn("val1", picked1, early_grouped[:, 3 * P :, :])
+        turn("val1", picked1, middle_grouped[:, :P, :])
 
         wval_rows = wval.rearrange("(p t) c -> p t c", t=PACK)
         wval_raw = []
-        for first, last, reuse in ((0, 1, "prob0"), (1, 3, "rows1"), (3, 4, "prob1")):
+        for first, last, reuse in ((0, 1, "prob0"), (1, 3, "rows0"), (3, 4, "prob1")):
             piece = sbuf("wval_raw%d" % first, [P, PACK, (last - first) * P], F32, reuse)
             nc.sync.dma_start(out=piece[:], in_=wval_rows[:, :, first * P : last * P])
             wval_raw.extend(piece[:, :, b * P : (b + 1) * P] for b in range(last - first))
 
-        turn("val2", pick_values(2, I, "denom"), grouped2[:])
+        turn("val2", pick_values(2, I, "denom"), middle_grouped[:, P:, :])
         mid_mx = quantized("early", early_grouped[:], 2 * WINDOW)
         window_weights, memory_weights = columns_of(mid_mx, 0), columns_of(mid_mx, Q)
         picked3 = pick_values(3, LAST_GATHER_VECTOR_SLOTS, "picked_words")
@@ -189,8 +189,8 @@ def tile_attend_knn_memory_kernel(tc, query, wkey, wval, keys_words, keys_scales
         interleave(nc.scalar.copy, first_grouped[:], wval_raw[0])
         grouped3 = sbuf("val_grouped3", [P, P, PACK], BF16, "prob0")
         turn("val3", picked3, grouped3[:])
-        val_mx = [columns_of(mid_mx, (2 + b) * P) for b in range(2)]
-        val_mx.append(quantized("val2", grouped2[:], "key_words"))
+        middle_mx = quantized("middle", middle_grouped[:], "key_words")
+        val_mx = [columns_of(mid_mx, 2 * P), columns_of(middle_mx, 0), columns_of(middle_mx, P)]
 
         second_grouped = sbuf("wval_grouped1", [P, P, PACK], BF16)
         third_grouped = sbuf("wval_grouped2", [P, P, PACK], BF16)
@@ -202,8 +202,8 @@ def tile_attend_knn_memory_kernel(tc, query, wkey, wval, keys_words, keys_scales
         cut = LAST_PIECE_VECTOR_COLUMNS
         interleave(nc.vector.tensor_copy, last_grouped[:, :cut, :], wval_raw[3][:, :, :cut])
         interleave(nc.scalar.copy, last_grouped[:, cut:, :], wval_raw[3][:, :, cut:])
-        val_mx.append(quantized("val3", grouped3[:]))
         wval_mx.append(quantized("wval2", third_grouped[:]))
+        val_mx.append(quantized("val3", grouped3[:]))
         wval_mx.append(quantized("wval3", last_grouped[:]))
 
         result = sbuf("result", [P, E], F32, "prob1")

from contextlib import ExitStack

import concourse.mybir as mybir
from concourse.masks import make_identity

D, T, I, Q, E, M = 512, 2048, 512, 128, 512, 512
FLOPS = 2 * Q * (D * M + D * I + M * E + I * E)

F32 = mybir.dt.float32
BF16 = mybir.dt.bfloat16
I32 = mybir.dt.int32
U32 = mybir.dt.uint32
U16 = mybir.dt.uint16
U8 = mybir.dt.uint8
FP8X4 = mybir.dt.float8_e4m3fn_x4
ALU = mybir.AluOpType
ACT = mybir.ActivationFunctionType

P = 128
PACK = 4
WINDOW = T * 4
BLOCKS = E // P
WKEY_VECTOR_COLUMNS = 288
LAST_GATHER_VECTOR_SLOTS = 320
LAST_PIECE_VECTOR_COLUMNS = 48


def interleave(copy, dst, src):
    copy(out=dst.rearrange("p (c i) t -> p c t i", i=4), in_=src.rearrange("p t (c i) -> p c t i", i=4))


def tile_attend_knn_memory_kernel(tc, query, wkey, wval, keys_words, keys_scales, vals, gb, msz, size, offs, out):
    nc = tc.nc
    with ExitStack() as ctx:
        keep = ctx.enter_context(tc.tile_pool(name="keep", bufs=1))
        shared = ctx.enter_context(tc.tile_pool(name="shared", bufs=1))
        psum = ctx.enter_context(tc.psum_pool(name="psum", bufs=1))

        def sbuf(name, shape, dtype, reuse=None):
            if isinstance(reuse, int):
                return shared.tile(shape, dtype, name=name, offset=reuse, align_bytes=256)
            return keep.tile(shape, dtype, name=name, tag=reuse or name, align_bytes=256)

        def quantized(name, grouped, reuse=None):
            width = grouped.shape[1]
            codes = sbuf(name + "_codes", [P, width], U32, reuse)
            scales = sbuf(name + "_scales", [P, width], U8)
            nc.vector.quantize_mx(out=codes[:].bitcast(FP8X4), scales=scales[:], in_=grouped.rearrange("p c t -> p (c t)"))
            return codes[:], scales[:]

        def columns_of(operand, first, width=P):
            return operand[0][:, first : first + width], operand[1][:, first : first + width]

        def product(acc, stationary, moving, start, stop):
            nc.tensor.matmul_mx(
                out=acc, lhsT=stationary[0].bitcast(FP8X4), lhsT_scale=stationary[1],
                rhs=moving[0].bitcast(FP8X4), rhs_scale=moving[1], start=start, stop=stop,
            )

        key_bytes = sbuf("key_bytes", [P, T], U8, 0)
        nc.gpsimd.memset(key_bytes[:].bitcast(I32), 0)
        vectors = sbuf("vectors", [P, P], F32)
        nc.vector.memset(vectors[:], 0.0)
        ident = sbuf("ident", [P, P], F32)
        make_identity(nc, ident[:])

        q_raw = sbuf("q_raw", [P, PACK, Q], F32)
        nc.sync.dma_start(out=q_raw[:], in_=query.rearrange("(p t) c -> p t c", t=PACK))
        offsets = keep.tile([P, I // 16], U16, name="offsets")
        nc.sync.dma_start(offsets[:], offs)
        nc.sync.dma_start(out=key_bytes[0:P:8, :].bitcast(I32), in_=keys_scales[0].bitcast(I32))
        wkey_raw = sbuf("wkey_raw", [P, PACK, M], F32, WINDOW)
        nc.sync.dma_start(out=wkey_raw[:], in_=wkey.rearrange("(p t) c -> p t c", t=PACK))
        nc.sync.dma_start(out=vectors[0:1, :], in_=gb.rearrange("q o -> o q"))
        nc.sync.dma_start(out=vectors[4:8, :], in_=msz.rearrange("o (b c) -> (o b) c", c=P))
        nc.sync.dma_start(out=vectors[8:12, :], in_=size.rearrange("o (b c) -> (o b) c", c=P))
        key_words = sbuf("key_words", [P, T], U32)
        nc.sync.dma_start(
            out=key_words[:].bitcast(I32), in_=keys_words[0].rearrange("p n t -> p (n t)").bitcast(I32)
        )

        picked_bytes = sbuf("picked_bytes", [P, I], U8)
        nc.vector.tensor_copy(picked_bytes[:], key_bytes[:].indirect(offsets[:]))
        key_plane = sbuf("key_plane", [P, I], U8)
        nc.vector.tensor_copy(key_plane[:].bitcast(I32), picked_bytes[:].bitcast(I32))
        for row in range(1, 4):
            nc.sync.dma_start(out=key_plane[row:P:32, :].bitcast(I32), in_=picked_bytes[8 * row : P : 32, :].bitcast(I32))

        def load_values(b, reuse):
            raw = sbuf("val_raw%d" % b, [P, T], F32, reuse)
            nc.sync.dma_start(out=raw[:], in_=vals[b * P : (b + 1) * P, :])
            return raw

        val_raw = {0: load_values(0, 0)}

        q_grouped = sbuf("q_grouped", [P, Q, PACK], BF16)
        interleave(nc.scalar.copy, q_grouped[:], q_raw[:])
        q_mx = quantized("q", q_grouped[:])
        wkey_grouped = sbuf("wkey_grouped", [P, M, PACK], BF16, 2 * WINDOW)
        cut = WKEY_VECTOR_COLUMNS
        interleave(nc.vector.tensor_copy, wkey_grouped[:, :cut, :], wkey_raw[:, :, :cut])
        interleave(nc.scalar.copy, wkey_grouped[:, cut:, :], wkey_raw[:, :, cut:])
        val_raw[1] = load_values(1, WINDOW)
        vectors_turned = psum.tile([P, P], F32, name="vectors_turned", tag="scores0")
        nc.tensor.transpose(vectors_turned[:], vectors[:], ident[:])
        columns = sbuf("columns", [P, 12], F32)
        nc.vector.tensor_copy(columns[:], vectors_turned[:, 0:12])
        gate_exp = sbuf("gate_exp", [P, 2], F32)
        nc.scalar.activation(gate_exp[:, 0:1], columns[:, 0:1], ACT.Exp)
        nc.scalar.activation(gate_exp[:, 1:2], columns[:, 0:1], ACT.Exp, scale=-1.0)
        spreads = []
        for s in range(2):
            spread = psum.tile([P, PACK, P], F32, name="spread%d" % s, tag="spread%d" % s)
            for t in range(PACK):
                column = 4 * (s + 1) + t
                nc.tensor.transpose(spread[:, t, :], columns[:, column : column + 1].to_broadcast([P, P]), ident[:])
            spreads.append(spread)

        wkey_mx = quantized("wkey", wkey_grouped[:], "vectors")
        val_raw[2] = load_values(2, 2 * WINDOW)
        picked_words = sbuf("picked_words", [P, I], U32)
        nc.vector.tensor_copy(picked_words[:], key_words[:].indirect(offsets[:]))

        denom = sbuf("denom", [P, 2], F32)
        probs = []
        for s, keys_mx in enumerate((wkey_mx, (picked_words[:], key_plane[:]))):
            scores = psum.tile([P, M], F32, name="scores%d" % s, tag="scores%d" % s)
            product(scores[:], q_mx, keys_mx, True, True)
            neg_max = sbuf("neg_max%d" % s, [P, 1], F32, "key_words" if s == 0 else None)
            nc.vector.tensor_reduce(neg_max[:], scores[:], mybir.AxisListType.X, ALU.max, negate=True)
            prob = sbuf("prob%d" % s, [P, M], F32)
            total = sbuf("total%d" % s, [P, 1], F32)
            nc.scalar.activation(prob[:], scores[:], ACT.Exp, bias=neg_max[:], scale=1.0, accum_out=total[:])
            nc.scalar.activation(denom[:, s : s + 1], total[:], ACT.Identity, scale=gate_exp[:, s : s + 1], bias=total[:])
            probs.append(prob)
        val_raw[3] = load_values(3, "key_words")

        def turn(name, rows, grouped, copy=nc.scalar.copy):
            words = rows[:].bitcast(F32)
            turned = psum.tile([P, 2, P], F32, name=name + "_turned", tag="turned", bufs=4)
            for u in range(2):
                nc.tensor.transpose(turned[:, u, :], words[:, u : 2 * P : 2], ident[:])
            copy(
                out=grouped.rearrange("p c t -> p (c t)").bitcast(F32).rearrange("p (c u) -> p c u", u=2),
                in_=turned[:].rearrange("p u c -> p c u"),
            )

        def pick_values(b, vector_slots, reuse):
            picked = sbuf("picked%d" % b, [P, I], BF16, reuse)
            cut = vector_slots // 16
            if vector_slots > 0:
                nc.vector.tensor_copy(picked[:, :vector_slots], val_raw[b][:].indirect(offsets[:, :cut]))
            if vector_slots < I:
                nc.scalar.activation(picked[:, vector_slots:], val_raw[b][:].indirect(offsets[:, cut:]), ACT.Copy)
            return picked

        picked0 = pick_values(0, I, "picked_words")
        early_grouped = sbuf("early_grouped", [P, 3 * P, PACK], BF16, WINDOW)
        middle_grouped = sbuf("middle_grouped", [P, 2 * P, PACK], BF16)
        weight_rows = []
        factor = sbuf("factor", [P, 2], F32, 0)
        for s in range(2):
            nc.vector.reciprocal(factor[:, s : s + 1], denom[:, s : s + 1])
            rows = sbuf("rows%d" % s, [P, M], BF16)
            nc.vector.scalar_tensor_tensor(
                out=rows[:], in0=probs[s][:], scalar=factor[:, s : s + 1],
                in1=spreads[s][:].rearrange("p b c -> p (b c)"), op0=ALU.mult, op1=ALU.mult,
            )
            weight_rows.append(rows)

        picked1 = pick_values(1, 0, "total1")
        turn("val0", picked0, early_grouped[:, 2 * P :, :], nc.vector.tensor_copy)
        for s in range(2):
            turn("rows%d" % s, weight_rows[s], early_grouped[:, s * Q : (s + 1) * Q, :])
        turn("val1", picked1, middle_grouped[:, :P, :])

        wval_rows = wval.rearrange("(p t) c -> p t c", t=PACK)
        wval_raw = []
        for first, last, reuse in ((0, 1, "prob0"), (1, 3, "rows0"), (3, 4, "prob1")):
            piece = sbuf("wval_raw%d" % first, [P, PACK, (last - first) * P], F32, reuse)
            nc.sync.dma_start(out=piece[:], in_=wval_rows[:, :, first * P : last * P])
            wval_raw.extend(piece[:, :, b * P : (b + 1) * P] for b in range(last - first))

        turn("val2", pick_values(2, I, "denom"), middle_grouped[:, P:, :])
        mid_mx = quantized("early", early_grouped[:], 2 * WINDOW)
        window_weights, memory_weights = columns_of(mid_mx, 0), columns_of(mid_mx, Q)
        picked3 = pick_values(3, LAST_GATHER_VECTOR_SLOTS, "picked_words")
        first_grouped = sbuf("wval_grouped0", [P, P, PACK], BF16)
        interleave(nc.scalar.copy, first_grouped[:], wval_raw[0])
        grouped3 = sbuf("val_grouped3", [P, P, PACK], BF16, "prob0")
        turn("val3", picked3, grouped3[:])
        middle_mx = quantized("middle", middle_grouped[:], "key_words")
        val_mx = [columns_of(mid_mx, 2 * P), columns_of(middle_mx, 0), columns_of(middle_mx, P)]

        second_grouped = sbuf("wval_grouped1", [P, P, PACK], BF16)
        third_grouped = sbuf("wval_grouped2", [P, P, PACK], BF16)
        last_grouped = sbuf("wval_grouped3", [P, P, PACK], BF16)
        wval_mx = [quantized("wval0", first_grouped[:])]
        interleave(nc.vector.tensor_copy, second_grouped[:], wval_raw[1])
        interleave(nc.vector.tensor_copy, third_grouped[:], wval_raw[2])
        wval_mx.append(quantized("wval1", second_grouped[:]))
        cut = LAST_PIECE_VECTOR_COLUMNS
        interleave(nc.vector.tensor_copy, last_grouped[:, :cut, :], wval_raw[3][:, :, :cut])
        interleave(nc.scalar.copy, last_grouped[:, cut:, :], wval_raw[3][:, :, cut:])
        wval_mx.append(quantized("wval2", third_grouped[:]))
        val_mx.append(quantized("val3", grouped3[:]))
        wval_mx.append(quantized("wval3", last_grouped[:]))

        result = sbuf("result", [P, E], F32, "prob1")
        for b, bank in enumerate(("scores0", "scores1", "spread0", "spread1")):
            cols = slice(b * P, (b + 1) * P)
            acc = psum.tile([P, P], F32, name="acc%d" % b, tag=bank)
            product(acc[:], memory_weights, val_mx[b], True, False)
            product(acc[:], window_weights, wval_mx[b], False, True)
            (nc.vector.tensor_copy if b == BLOCKS - 1 else nc.scalar.copy)(out=result[:, cols], in_=acc[:])
            if b > 0:
                stored = slice(0 if b == 1 else b * P, (b + 1) * P)
                nc.sync.dma_start(out=out[:, stored], in_=result[:, stored])
